import numpy as np
import ml_dtypes


def mxq(x, axis, fmt="e4m3"):
    dtype, down = {"e4m3": (ml_dtypes.float8_e4m3fn, 7), "e5m2": (ml_dtypes.float8_e5m2, 14)}[fmt]
    v = np.moveaxis(np.asarray(x, np.float32).astype(ml_dtypes.bfloat16).astype(np.float64), axis, -1)
    blocks = v.reshape(v.shape[:-1] + (-1, 32))
    amax = np.abs(blocks).max(-1, keepdims=True)
    byte = np.maximum(np.where(amax > 0, np.frexp(amax)[1] - 1 + 127, 0) - down, 1)
    scale = np.exp2(byte - 127.0)
    codes = (blocks / scale).astype(np.float32).astype(dtype).astype(np.float64)
    return np.moveaxis((codes * scale).reshape(v.shape), -1, axis)


WIDE = False


def mx_kscale(k):
    if not WIDE:
        return np.ones(k)
    levels = np.array([24, -24, 12, -12, 0])
    if k % 512:
        return np.exp2(np.random.permutation(np.resize(levels, k // 32))).repeat(32)
    a = np.empty((k // 512, 16))
    for p in range(k // 512):
        a[p, :8] = np.random.permutation(np.resize(levels, 8))
        for g in range(8):
            far = levels[np.abs(levels - a[p, g]) >= 10]
            a[p, g + 8] = far[np.random.randint(len(far))]
    return np.exp2(a.ravel()).repeat(32)


def f64(x):
    return np.asarray(x).astype(np.float64)


def striped8(idx):
    return np.concatenate([v.reshape(-1, 16).T for v in idx]).astype(np.uint16)


def unstriped8(offs):
    return np.stack([offs[16 * g:16 * g + 16].T.reshape(-1) for g in range(8)]).astype(np.int64)


E2M1 = np.array([0.0, 0.5, 1.0, 1.5, 2.0, 3.0, 4.0, 6.0, -0.0, -0.5, -1.0, -1.5, -2.0, -3.0, -4.0, -6.0])


def pack_weight(w, fmt):
    k, n = w.shape
    w = f64(np.asarray(w, np.float32).astype(ml_dtypes.bfloat16)).reshape(k // 32, 32, n)
    amax = np.abs(w).max(1)
    if fmt == "e4m3":
        byte = np.frexp(amax)[1] - 1 + 127 - 7
    else:
        mant, ex = np.frexp(amax / 6.0)
        byte = np.where(mant > 0.5, ex, ex - 1) + 127
    byte = np.clip(np.where(amax > 0, byte, 1), 1, 254)
    scaled = (w * np.exp2(127.0 - byte)[:, None, :]).reshape(k, n).astype(np.float32)
    by_word = np.ascontiguousarray(scaled.reshape(k // 512, 128, 4, n).transpose(0, 1, 3, 2))
    if fmt == "e4m3":
        words = by_word.astype(ml_dtypes.float8_e4m3fn).view(np.uint8)
    else:
        c = by_word.astype(ml_dtypes.float4_e2m1fn).view(np.uint8) & 0xF
        words = (c[..., 0::2] | (c[..., 1::2] << 4)).reshape(k // 512, 128, 2 * n)
    return np.ascontiguousarray(words), np.ascontiguousarray(byte.astype(np.uint8).reshape(k // 512, 16, n))


def unpack_weight(words, scales, fmt):
    g, _, n = scales.shape
    words = np.ascontiguousarray(words).reshape(g, 128, n, -1)
    if fmt == "e4m3":
        vals = words.view(ml_dtypes.float8_e4m3fn).astype(np.float64)
    else:
        nib = np.empty((g, 128, n, 4), np.uint8)
        nib[..., 0::2] = words & 0xF
        nib[..., 1::2] = words >> 4
        vals = E2M1[nib]
    vals = vals * np.repeat(np.exp2(scales.astype(np.float64) - 127.0), 8, axis=1)[..., None]
    return vals.transpose(0, 1, 3, 2).reshape(g * 512, n)


def planes(y):
    n, m = y.shape
    v = y.astype(np.float32).astype(ml_dtypes.bfloat16).astype(np.float64).reshape(n // 32, 32, m)
    top = np.abs(v).max(1)
    byte = np.clip(np.where(top > 0, np.frexp(top)[1] - 1 + 127 - 7, 1), 1, 254)
    codes = (v * np.exp2(127.0 - byte)[:, None, :]).reshape(n, m).astype(np.float32).astype(ml_dtypes.float8_e4m3fn).view(np.uint8)
    words = codes.reshape(n // 512, 128, 4, m).transpose(0, 1, 3, 2)
    return np.ascontiguousarray(words), np.ascontiguousarray(byte.astype(np.uint8).reshape(n // 512, 16, m))


K, R, N, T, J = 512, 1024, 512, 2048, 1024


def setup_inputs():
    n = np.random.standard_normal
    s = mx_kscale(K)[:, None]
    u = mx_kscale(R)[:, None]
    wd = n((R, N)) / np.sqrt(R) / u
    p_wu = pack_weight(n((K, R)) / np.sqrt(K) / s * u.T, "e4m3")
    p_wd8 = pack_weight(wd[:512], "e4m3")
    p_wd4 = pack_weight(wd[512:], "e2m1")
    return {
        "xT": (n((K, T)) * s).astype(np.float32),
        "wgt": np.repeat(np.random.uniform(0.5, 2.0, (8, J)), 16, axis=0).astype(np.float32),
        "wg": (n((K, R)) / np.sqrt(K) / s).astype(np.float32),
        "wu_words": p_wu[0],
        "wu_scales": p_wu[1],
        "wd8_words": p_wd8[0],
        "wd8_scales": p_wd8[1],
        "wd4_words": p_wd4[0],
        "wd4_scales": p_wd4[1],
        "offs": striped8(np.stack([np.random.permutation(T)[:J] for _ in range(8)])),
    }


def reference(xT, wgt, wg, wu_words, wu_scales, wd8_words, wd8_scales, wd4_words, wd4_scales, offs):
    idx = unstriped8(offs)
    rows = np.arange(K)
    xg = f64(wgt)[rows // 4 % 128] * f64(xT)[rows[:, None], idx[rows % 512 // 64]]
    xT_ = mxq(xg, 0, "e4m3")
    wg_ = mxq(f64(wg), 0, "e4m3")
    wu_ = unpack_weight(wu_words, wu_scales, "e4m3")
    ga = wg_.T @ xT_
    ub = wu_.T @ xT_
    h = np.maximum(ga, 0.0) * ub
    h_ = mxq(h, 0, "e4m3")
    wd8_ = unpack_weight(wd8_words, wd8_scales, "e4m3")
    wd4_ = unpack_weight(wd4_words, wd4_scales, "e2m1")
    y = wd8_.T @ h_[:512] + wd4_.T @ h_[512:]
    return (y,) + planes(y)

@@ -1,0 +1,276 @@
+from contextlib import ExitStack
+
+import concourse.mybir as mybir
+
+K, R, N, T, J = 512, 1024, 512, 2048, 1024
+FLOPS = 2 * K * R * J * 2 + 2 * R * N * J
+
+F32 = mybir.dt.float32
+BF16 = mybir.dt.bfloat16
+I32 = mybir.dt.int32
+U32 = mybir.dt.uint32
+U16 = mybir.dt.uint16
+U8 = mybir.dt.uint8
+FP8X4 = mybir.dt.float8_e4m3fn_x4
+FP4X4 = mybir.dt.float4_e2m1fn_x4
+MULT = mybir.AluOpType.mult
+RELU = mybir.ActivationFunctionType.Relu
+
+P = 128
+PACK = 4
+PASS = P * PACK
+CH = 256
+NCH = J // CH
+SUB = 128
+
+
+def tile_list_relu_mix_noneP_kernel(
+    tc, xT, wgt, wg, wu_words, wu_scales, wd8_words, wd8_scales, wd4_words, wd4_scales, offs, out_0, out_1, out_2
+):
+    nc = tc.nc
+    with ExitStack() as ctx:
+        keep = ctx.enter_context(tc.tile_pool(name="keep", bufs=1))
+        ring = ctx.enter_context(tc.tile_pool(name="ring", bufs=3))
+        ps_ga = ctx.enter_context(tc.psum_pool(name="ps_ga", bufs=2))
+        ps_ub = ctx.enter_context(tc.psum_pool(name="ps_ub", bufs=3))
+        ps_y = ctx.enter_context(tc.psum_pool(name="ps_y", bufs=3))
+
+        offsets = keep.tile([P, J // 16], U16, name="offsets")
+        nc.sync.dma_start(offsets[:], offs)
+        wgt_sb = keep.tile([P, J], F32, name="wgt_sb")
+        nc.sync.dma_start(out=wgt_sb[:], in_=wgt)
+        x_rows = xT.rearrange("(p i) t -> p i t", i=PACK)
+        x_sb = [keep.tile([P, T], F32, name="x_sb%d" % i, tag="x%d" % i, align_bytes=64) for i in range(PACK)]
+        wu_sraw = keep.tile([P, PASS], U8, name="wu_sraw")
+        nc.vector.memset(wu_sraw[:].bitcast(I32), 0)
+        wu_sc = wu_scales[0].bitcast(I32).rearrange("q (b w) -> b q w", b=2)
+        nc.sync.dma_start(out=x_sb[0][:], in_=x_rows[:, 0, :])
+        for q in range(4):
+            nc.sync.dma_start(out=wu_sraw[32 * q : 32 * q + 8, :].bitcast(I32), in_=wu_sc[:, 4 * q : 4 * q + 4, :])
+        for i in range(1, PACK):
+            nc.sync.dma_start(out=x_sb[i][:], in_=x_rows[:, i, :])
+
+        wg_rows = wg.rearrange("(p i) r -> p i r", i=PACK)
+        wg_raw = [keep.tile([P, PACK, PASS], F32, name="wg_raw%d" % b) for b in range(2)]
+        wu_raw = keep.tile([P, R], U32, name="wu_raw")
+        wd8_raw = keep.tile([P, N], U32, name="wd8_raw")
+        wd4_raw = keep.tile([P, N], U16, name="wd4_raw")
+        nc.sync.dma_start(out=wg_raw[0][:], in_=wg_rows[:, :, 0:PASS])
+        nc.sync.dma_start(out=wu_raw[:].bitcast(I32), in_=wu_words[0].rearrange("p r i -> p (r i)").bitcast(I32))
+        nc.sync.dma_start(out=wg_raw[1][:], in_=wg_rows[:, :, PASS:R])
+        nc.sync.dma_start(out=wd8_raw[:].bitcast(I32), in_=wd8_words[0].rearrange("p n i -> p (n i)").bitcast(I32))
+        nc.sync.dma_start(out=wd4_raw[:].bitcast(I32), in_=wd4_words[0].bitcast(I32))
+
+        wd_sraw = keep.tile([P, N], U8, name="wd_sraw")
+        nc.gpsimd.memset(wd_sraw[:].bitcast(I32), 0)
+        for q in range(4):
+            nc.gpsimd.dma_start(
+                out=wd_sraw[32 * q : 32 * q + 4, :].bitcast(I32), in_=wd4_scales[0].bitcast(I32)[4 * q : 4 * q + 4, :]
+            )
+            nc.gpsimd.dma_start(
+                out=wd_sraw[32 * q + 4 : 32 * q + 8, :].bitcast(I32), in_=wd8_scales[0].bitcast(I32)[4 * q : 4 * q + 4, :]
+            )
+
+        picked = [keep.tile([P, PACK, CH], F32, name="picked%d" % c) for c in range(NCH)]
+        xg_bf = [keep.tile([P, CH * PACK], BF16, name="xg_bf%d" % c, align_bytes=64) for c in range(NCH)]
+        xg_codes = [keep.tile([P, CH], U32, name="xg_codes%d" % c, align_bytes=64) for c in range(NCH)]
+        xg_scale = [keep.tile([P, CH], U8, name="xg_scale%d" % c, align_bytes=64) for c in range(NCH)]
+
+        def gather(i, c):
+            nc.vector.tensor_tensor(
+                picked[c][:, i, :],
+                x_sb[i][:].indirect(offsets[:, c * (CH // 16) : (c + 1) * (CH // 16)]),
+                wgt_sb[:, c * CH : (c + 1) * CH],
+                MULT,
+            )
+
+        def weave_x(c):
+            nc.scalar.copy(
+                out=xg_bf[c][:].rearrange("p (g e i) -> p g i e", e=4, i=PACK),
+                in_=picked[c][:].rearrange("p i (g e) -> p g i e", e=4),
+            )
+
+        def quant_x(c):
+            nc.vector.quantize_mx(out=xg_codes[c][:].bitcast(FP8X4), scales=xg_scale[c][:], in_=xg_bf[c][:])
+
+        wg_bf = [keep.tile([P, PASS * PACK], BF16, name="wg_bf%d" % b, align_bytes=64) for b in range(2)]
+        wg_codes = [keep.tile([P, PASS], U32, name="wg_codes%d" % b, align_bytes=64) for b in range(2)]
+        wg_scale = [keep.tile([P, PASS], U8, name="wg_scale%d" % b, align_bytes=64) for b in range(2)]
+        wu_codes = keep.tile([P, R], U32, name="wu_codes", align_bytes=64)
+        wu_scale = keep.tile([P, PASS], U8, name="wu_scale", align_bytes=64)
+        wd8_codes = keep.tile([P, N], U32, name="wd8_codes", align_bytes=64)
+        wd4_codes = keep.tile([P, N], U16, name="wd4_codes", align_bytes=64)
+
+        def weave_wg(b, copy):
+            copy(
+                out=wg_bf[b][:].rearrange("p (t m i) -> p m i t", t=PACK, i=PACK),
+                in_=wg_raw[b][:].rearrange("p i (m t) -> p m i t", t=PACK),
+            )
+
+        def quant_wg(b):
+            nc.vector.quantize_mx(out=wg_codes[b][:].bitcast(FP8X4), scales=wg_scale[b][:], in_=wg_bf[b][:])
+
+        def deal(copy, dst, src):
+            copy(
+                out=dst.rearrange("p (b t m) -> p b m t", t=PACK, m=P),
+                in_=src.rearrange("p (b m t) -> p b m t", t=PACK, m=P),
+            )
+
+        h_bf = {}
+        h_codes = {}
+        h_scale = {}
+
+        def up(c, b, s):
+            if s == 0:
+                h_bf[c, b] = keep.tile([P, CH * PACK], BF16, name="h_bf%d_%d" % (c, b), align_bytes=64)
+            cols = slice(s * SUB, (s + 1) * SUB)
+            ga = ps_ga.tile([P, PACK, SUB], F32, name="ga")
+            ub = ps_ub.tile([P, PACK, SUB], F32, name="ub")
+            for t in range(PACK):
+                nc.tensor.matmul_mx(
+                    out=ga[:, t, :],
+                    lhsT=wg_codes[b][:, t * P : (t + 1) * P].bitcast(FP8X4),
+                    lhsT_scale=wg_scale[b][:, t * P : (t + 1) * P],
+                    rhs=xg_codes[c][:, cols].bitcast(FP8X4),
+                    rhs_scale=xg_scale[c][:, cols],
+                    start=True,
+                    stop=True,
+                )
+            for t in range(PACK):
+                nc.tensor.matmul_mx(
+                    out=ub[:, t, :],
+                    lhsT=wu_codes[:, b * PASS + t * P : b * PASS + (t + 1) * P].bitcast(FP8X4),
+                    lhsT_scale=wu_scale[4 * b : P, t * P : (t + 1) * P],
+                    rhs=xg_codes[c][:, cols].bitcast(FP8X4),
+                    rhs_scale=xg_scale[c][:, cols],
+                    start=True,
+                    stop=True,
+                )
+            gate = ring.tile([P, SUB, PACK], F32, name="gate")
+            nc.scalar.activation(out=gate[:], in_=ga[:].rearrange("p t j -> p j t"), func=RELU)
+            nc.vector.tensor_tensor(
+                h_bf[c, b][:, s * SUB * PACK : (s + 1) * SUB * PACK].rearrange("p (j t) -> p j t", t=PACK),
+                ub[:].rearrange("p t j -> p j t"),
+                gate[:],
+                MULT,
+            )
+
+        def quant_h(c, b):
+            h_codes[c, b] = keep.tile([P, CH], U32, name="h_codes%d_%d" % (c, b), align_bytes=64)
+            h_scale[c, b] = keep.tile([P, CH], U8, name="h_scale%d_%d" % (c, b), align_bytes=64)
+            nc.vector.quantize_mx(out=h_codes[c, b][:].bitcast(FP8X4), scales=h_scale[c, b][:], in_=h_bf[c, b][:])
+
+        y_rows = out_0.rearrange("(p t) j -> p t j", t=PACK)
+        y_words = out_1[0].rearrange("p j i -> p (j i)").bitcast(I32)
+        y_scale = keep.tile([P, J], U8, name="y_scale", align_bytes=64)
+        y_sb = {}
+
+        def down(c):
+            y_sb[c] = keep.tile([P, PACK, CH], F32, name="y_sb%d" % c)
+            for u in range(2):
+                acc = ps_y.tile([P, 2, CH], F32, name="acc")
+                for e in range(2):
+                    t = 2 * u + e
+                    nc.tensor.matmul_mx(
+                        out=acc[:, e, :],
+                        lhsT=wd8_codes[:, t * P : (t + 1) * P].bitcast(FP8X4),
+                        lhsT_scale=wd_scale[4:P, t * P : (t + 1) * P],
+                        rhs=h_codes[c, 0][:].bitcast(FP8X4),
+                        rhs_scale=h_scale[c, 0][:],
+                        start=True,
+                        stop=False,
+                    )
+                    nc.tensor.matmul_mx(
+                        out=acc[:, e, :],
+                        lhsT=wd4_codes[:, t * P : (t + 1) * P].bitcast(FP4X4),
+                        lhsT_scale=wd_scale[:, t * P : (t + 1) * P],
+                        rhs=h_codes[c, 1][:].bitcast(FP8X4),
+                        rhs_scale=h_scale[c, 1][:],
+                        start=False,
+                        stop=True,
+                    )
+                nc.scalar.copy(out=y_sb[c][:, 2 * u : 2 * u + 2, :], in_=acc[:])
+            nc.sync.dma_start(out=y_rows[:, :, c * CH : (c + 1) * CH], in_=y_sb[c][:])
+
+        y_bf = {}
+
+        def weave_y(c):
+            y_bf[c] = keep.tile([P, CH * PACK], BF16, name="y_bf%d" % c, align_bytes=64)
+            nc.vector.tensor_copy(
+                out=y_bf[c][:].rearrange("p (g e t) -> p g t e", e=4, t=PACK),
+                in_=y_sb[c][:].rearrange("p t (g e) -> p g t e", e=4),
+            )
+
+        def quant_y(c):
+            y_codes = keep.tile([P, CH], U32, name="y_codes%d" % c, align_bytes=64)
+            nc.vector.quantize_mx(
+                out=y_codes[:].bitcast(FP8X4), scales=y_scale[:, c * CH : (c + 1) * CH], in_=y_bf[c][:]
+            )
+            nc.sync.dma_start(out=y_words[:, c * CH : (c + 1) * CH], in_=y_codes[:].bitcast(I32))
+
+        for c in range(NCH):
+            gather(0, c)
+        deal(nc.vector.tensor_copy, wu_scale[:], wu_sraw[:])
+        for i in range(1, PACK - 1):
+            for c in range(NCH):
+                gather(i, c)
+        gather(3, 0)
+        weave_x(0)
+        gather(3, 1)
+        weave_x(1)
+        quant_x(0)
+        gather(3, 2)
+        weave_wg(0, nc.vector.tensor_copy)
+        gather(3, 3)
+        quant_wg(0)
+        deal(nc.vector.tensor_copy, wu_codes[:], wu_raw[:])
+        quant_x(1)
+        up(0, 0, 0)
+        weave_x(2)
+        up(0, 0, 1)
+        weave_wg(1, nc.scalar.copy)
+        up(1, 0, 0)
+        quant_h(0, 0)
+        quant_wg(1)
+        up(1, 0, 1)
+        deal(nc.scalar.copy, wd8_codes[:], wd8_raw[:])
+        deal(nc.scalar.copy, wd4_codes[:], wd4_raw[:])
+        wd_scale = keep.tile([P, N], U8, name="wd_scale", tag="x3", align_bytes=64)
+        deal(nc.vector.tensor_copy, wd_scale[:], wd_sraw[:])
+        up(0, 1, 0)
+        quant_h(1, 0)
+        quant_x(2)
+        up(0, 1, 1)
+        weave_x(3)
+        up(1, 1, 0)
+        quant_h(0, 1)
+        quant_x(3)
+        up(1, 1, 1)
+        down(0)
+        up(2, 0, 0)
+        quant_h(1, 1)
+        up(2, 0, 1)
+        down(1)
+        weave_y(0)
+        up(2, 1, 0)
+        quant_h(2, 0)
+        quant_y(0)
+        up(2, 1, 1)
+        weave_y(1)
+        up(3, 0, 0)
+        quant_h(2, 1)
+        quant_y(1)
+        up(3, 0, 1)
+        down(2)
+        up(3, 1, 0)
+        quant_h(3, 0)
+        up(3, 1, 1)
+        weave_y(2)
+        quant_h(3, 1)
+        quant_y(2)
+        down(3)
+        weave_y(3)
+        quant_y(3)
+        y_sc = out_2[0].bitcast(I32)
+        for q in range(4):
+            nc.sync.dma_start(out=y_sc[4 * q : 4 * q + 4, :], in_=y_scale[32 * q : 32 * q + 4, :].bitcast(I32))

@@ -19,9 +19,12 @@ RELU = mybir.ActivationFunctionType.Relu
 P = 128
 PACK = 4
 PASS = P * PACK
-CH = 256
-NCH = J // CH
+BANK = 512
 SUB = 128
+HALF = J // 2
+WIDTHS = [256, 256, 256, 128, 128]
+STARTS = [sum(WIDTHS[:c]) for c in range(len(WIDTHS))]
+NCH = len(WIDTHS)
 
 
 def tile_list_relu_mix_noneP_kernel(
@@ -36,58 +39,76 @@ def tile_list_relu_mix_noneP_kernel(
         ps_y = ctx.enter_context(tc.psum_pool(name="ps_y", bufs=3))
 
         offsets = keep.tile([P, J // 16], U16, name="offsets")
-        nc.sync.dma_start(offsets[:], offs)
-        wgt_sb = keep.tile([P, J], F32, name="wgt_sb")
-        nc.sync.dma_start(out=wgt_sb[:], in_=wgt)
+        wgt_sb = [keep.tile([P, HALF], F32, name="wgt_sb%d" % u) for u in range(2)]
         x_rows = xT.rearrange("(p i) t -> p i t", i=PACK)
-        x_sb = [keep.tile([P, T], F32, name="x_sb%d" % i, tag="x%d" % i, align_bytes=64) for i in range(PACK)]
-        wu_sraw = keep.tile([P, PASS], U8, name="wu_sraw")
-        nc.vector.memset(wu_sraw[:].bitcast(I32), 0)
-        wu_sc = wu_scales[0].bitcast(I32).rearrange("q (b w) -> b q w", b=2)
-        nc.sync.dma_start(out=x_sb[0][:], in_=x_rows[:, 0, :])
-        for q in range(4):
-            nc.sync.dma_start(out=wu_sraw[32 * q : 32 * q + 8, :].bitcast(I32), in_=wu_sc[:, 4 * q : 4 * q + 4, :])
-        for i in range(1, PACK):
-            nc.sync.dma_start(out=x_sb[i][:], in_=x_rows[:, i, :])
-
+        x_sb = [keep.tile([P, T], F32, name="x_sb%d" % i) for i in range(PACK)]
         wg_rows = wg.rearrange("(p i) r -> p i r", i=PACK)
-        wg_raw = [keep.tile([P, PACK, PASS], F32, name="wg_raw%d" % b) for b in range(2)]
-        wu_raw = keep.tile([P, R], U32, name="wu_raw")
+        wg_raw = [[keep.tile([P, PACK, PASS // 2], F32, name="wg_raw%d_%d" % (b, u)) for u in range(2)] for b in range(2)]
+        wu_raw = [keep.tile([P, PASS], U32, name="wu_raw%d" % b) for b in range(2)]
         wd8_raw = keep.tile([P, N], U32, name="wd8_raw")
         wd4_raw = keep.tile([P, N], U16, name="wd4_raw")
-        nc.sync.dma_start(out=wg_raw[0][:], in_=wg_rows[:, :, 0:PASS])
-        nc.sync.dma_start(out=wu_raw[:].bitcast(I32), in_=wu_words[0].rearrange("p r i -> p (r i)").bitcast(I32))
-        nc.sync.dma_start(out=wg_raw[1][:], in_=wg_rows[:, :, PASS:R])
+        wu_sraw = keep.tile([P, PASS], U8, name="wu_sraw")
+        wd_sraw = keep.tile([P, N], U8, name="wd_sraw")
+        nc.vector.memset(wu_sraw[:].bitcast(I32), 0)
+        nc.vector.memset(wd_sraw[:].bitcast(I32), 0)
+
+        def load_wg(b, u):
+            first = b * PASS + u * (PASS // 2)
+            nc.sync.dma_start(out=wg_raw[b][u][:], in_=wg_rows[:, :, first : first + PASS // 2])
+
+        wu_src = wu_words[0].rearrange("p r i -> p (r i)").bitcast(I32)
+        wu_sc = wu_scales[0].bitcast(I32).rearrange("q (b w) -> b q w", b=2)
+        nc.sync.dma_start(offsets[:], offs)
+        nc.sync.dma_start(out=wgt_sb[0][:], in_=wgt[:, 0:HALF])
+        nc.sync.dma_start(out=x_sb[0][:], in_=x_rows[:, 0, :])
+        nc.sync.dma_start(out=wgt_sb[1][:], in_=wgt[:, HALF:J])
+        nc.sync.dma_start(out=x_sb[1][:], in_=x_rows[:, 1, :])
+        for q in range(4):
+            nc.sync.dma_start(out=wu_sraw[32 * q : 32 * q + 8, :].bitcast(I32), in_=wu_sc[:, 4 * q : 4 * q + 4, :])
+        nc.sync.dma_start(out=x_sb[2][:], in_=x_rows[:, 2, :])
+        nc.sync.dma_start(out=wu_raw[0][:].bitcast(I32), in_=wu_src[:, 0:PASS])
+        nc.sync.dma_start(out=x_sb[3][:], in_=x_rows[:, 3, :])
+        load_wg(0, 0)
+        load_wg(0, 1)
+        nc.sync.dma_start(out=wu_raw[1][:].bitcast(I32), in_=wu_src[:, PASS:R])
+        load_wg(1, 0)
+        load_wg(1, 1)
         nc.sync.dma_start(out=wd8_raw[:].bitcast(I32), in_=wd8_words[0].rearrange("p n i -> p (n i)").bitcast(I32))
         nc.sync.dma_start(out=wd4_raw[:].bitcast(I32), in_=wd4_words[0].bitcast(I32))
-
-        wd_sraw = keep.tile([P, N], U8, name="wd_sraw")
-        nc.gpsimd.memset(wd_sraw[:].bitcast(I32), 0)
         for q in range(4):
-            nc.gpsimd.dma_start(
+            nc.sync.dma_start(
                 out=wd_sraw[32 * q : 32 * q + 4, :].bitcast(I32), in_=wd4_scales[0].bitcast(I32)[4 * q : 4 * q + 4, :]
             )
-            nc.gpsimd.dma_start(
+            nc.sync.dma_start(
                 out=wd_sraw[32 * q + 4 : 32 * q + 8, :].bitcast(I32), in_=wd8_scales[0].bitcast(I32)[4 * q : 4 * q + 4, :]
             )
 
-        picked = [keep.tile([P, PACK, CH], F32, name="picked%d" % c) for c in range(NCH)]
-        xg_bf = [keep.tile([P, CH * PACK], BF16, name="xg_bf%d" % c, align_bytes=64) for c in range(NCH)]
-        xg_codes = [keep.tile([P, CH], U32, name="xg_codes%d" % c, align_bytes=64) for c in range(NCH)]
-        xg_scale = [keep.tile([P, CH], U8, name="xg_scale%d" % c, align_bytes=64) for c in range(NCH)]
+        early = [keep.tile([P, 2, HALF], F32, name="early%d" % u) for u in range(2)]
+        late = [keep.tile([P, 2, w], F32, name="late%d" % c) for c, w in enumerate(WIDTHS)]
+        xg_bf = [keep.tile([P, w * PACK], BF16, name="xg_bf%d" % c, align_bytes=64) for c, w in enumerate(WIDTHS)]
+        xg_codes = [keep.tile([P, w], U32, name="xg_codes%d" % c, align_bytes=64) for c, w in enumerate(WIDTHS)]
+        xg_scale = [keep.tile([P, w], U8, name="xg_scale%d" % c, align_bytes=64) for c, w in enumerate(WIDTHS)]
 
-        def gather(i, c):
+        def gather(dst, i, first, width):
             nc.vector.tensor_tensor(
-                picked[c][:, i, :],
-                x_sb[i][:].indirect(offsets[:, c * (CH // 16) : (c + 1) * (CH // 16)]),
-                wgt_sb[:, c * CH : (c + 1) * CH],
+                dst,
+                x_sb[i][:].indirect(offsets[:, first // 16 : (first + width) // 16]),
+                wgt_sb[first // HALF][:, first % HALF : first % HALF + width],
                 MULT,
             )
 
-        def weave_x(c):
-            nc.scalar.copy(
-                out=xg_bf[c][:].rearrange("p (g e i) -> p g i e", e=4, i=PACK),
-                in_=picked[c][:].rearrange("p i (g e) -> p g i e", e=4),
+        def gather_early(i, u):
+            gather(early[u][:, i, :], i, u * HALF, HALF)
+
+        def gather_late(i, c):
+            gather(late[c][:, i - 2, :], i, STARTS[c], WIDTHS[c])
+
+        def weave_x(c, u, copy):
+            first = STARTS[c] % HALF
+            pair = late[c][:] if u else early[STARTS[c] // HALF][:, :, first : first + WIDTHS[c]]
+            copy(
+                out=xg_bf[c][:].rearrange("p (j i) -> p j i", i=PACK)[:, :, 2 * u : 2 * u + 2],
+                in_=pair.rearrange("p i j -> p j i"),
             )
 
         def quant_x(c):
@@ -96,25 +117,23 @@ def tile_list_relu_mix_noneP_kernel(
         wg_bf = [keep.tile([P, PASS * PACK], BF16, name="wg_bf%d" % b, align_bytes=64) for b in range(2)]
         wg_codes = [keep.tile([P, PASS], U32, name="wg_codes%d" % b, align_bytes=64) for b in range(2)]
         wg_scale = [keep.tile([P, PASS], U8, name="wg_scale%d" % b, align_bytes=64) for b in range(2)]
-        wu_codes = keep.tile([P, R], U32, name="wu_codes", align_bytes=64)
+        wu_codes = [keep.tile([P, PASS], U32, name="wu_codes%d" % b, align_bytes=64) for b in range(2)]
         wu_scale = keep.tile([P, PASS], U8, name="wu_scale", align_bytes=64)
         wd8_codes = keep.tile([P, N], U32, name="wd8_codes", align_bytes=64)
         wd4_codes = keep.tile([P, N], U16, name="wd4_codes", align_bytes=64)
+        wd_scale = keep.tile([P, N], U8, name="wd_scale", align_bytes=64)
 
-        def weave_wg(b, copy):
+        def weave_wg(b, u, copy):
             copy(
-                out=wg_bf[b][:].rearrange("p (t m i) -> p m i t", t=PACK, i=PACK),
-                in_=wg_raw[b][:].rearrange("p i (m t) -> p m i t", t=PACK),
+                out=wg_bf[b][:].rearrange("p (t m i) -> p m i t", t=PACK, i=PACK)[:, u * (P // 2) : (u + 1) * (P // 2)],
+                in_=wg_raw[b][u][:].rearrange("p i (m t) -> p m i t", t=PACK),
             )
 
         def quant_wg(b):
             nc.vector.quantize_mx(out=wg_codes[b][:].bitcast(FP8X4), scales=wg_scale[b][:], in_=wg_bf[b][:])
 
         def deal(copy, dst, src):
-            copy(
-                out=dst.rearrange("p (b t m) -> p b m t", t=PACK, m=P),
-                in_=src.rearrange("p (b m t) -> p b m t", t=PACK, m=P),
-            )
+            copy(out=dst.rearrange("p (t m) -> p m t", t=PACK), in_=src.rearrange("p (m t) -> p m t", t=PACK))
 
         h_bf = {}
         h_codes = {}
@@ -122,7 +141,7 @@ def tile_list_relu_mix_noneP_kernel(
 
         def up(c, b, s):
             if s == 0:
-                h_bf[c, b] = keep.tile([P, CH * PACK], BF16, name="h_bf%d_%d" % (c, b), align_bytes=64)
+                h_bf[c, b] = keep.tile([P, WIDTHS[c] * PACK], BF16, name="h_bf%d_%d" % (c, b), align_bytes=64)
             cols = slice(s * SUB, (s + 1) * SUB)
             ga = ps_ga.tile([P, PACK, SUB], F32, name="ga")
             ub = ps_ub.tile([P, PACK, SUB], F32, name="ub")
@@ -139,7 +158,7 @@ def tile_list_relu_mix_noneP_kernel(
             for t in range(PACK):
                 nc.tensor.matmul_mx(
                     out=ub[:, t, :],
-                    lhsT=wu_codes[:, b * PASS + t * P : b * PASS + (t + 1) * P].bitcast(FP8X4),
+                    lhsT=wu_codes[b][:, t * P : (t + 1) * P].bitcast(FP8X4),
                     lhsT_scale=wu_scale[4 * b : P, t * P : (t + 1) * P],
                     rhs=xg_codes[c][:, cols].bitcast(FP8X4),
                     rhs_scale=xg_scale[c][:, cols],
@@ -156,8 +175,8 @@ def tile_list_relu_mix_noneP_kernel(
             )
 
         def quant_h(c, b):
-            h_codes[c, b] = keep.tile([P, CH], U32, name="h_codes%d_%d" % (c, b), align_bytes=64)
-            h_scale[c, b] = keep.tile([P, CH], U8, name="h_scale%d_%d" % (c, b), align_bytes=64)
+            h_codes[c, b] = keep.tile([P, WIDTHS[c]], U32, name="h_codes%d_%d" % (c, b), align_bytes=64)
+            h_scale[c, b] = keep.tile([P, WIDTHS[c]], U8, name="h_scale%d_%d" % (c, b), align_bytes=64)
             nc.vector.quantize_mx(out=h_codes[c, b][:].bitcast(FP8X4), scales=h_scale[c, b][:], in_=h_bf[c, b][:])
 
         y_rows = out_0.rearrange("(p t) j -> p t j", t=PACK)
@@ -166,13 +185,14 @@ def tile_list_relu_mix_noneP_kernel(
         y_sb = {}
 
         def down(c):
-            y_sb[c] = keep.tile([P, PACK, CH], F32, name="y_sb%d" % c)
-            for u in range(2):
-                acc = ps_y.tile([P, 2, CH], F32, name="acc")
-                for e in range(2):
-                    t = 2 * u + e
+            width = WIDTHS[c]
+            share = BANK // width
+            y_sb[c] = keep.tile([P, PACK, width], F32, name="y_sb%d" % c)
+            for first in range(0, PACK, share):
+                acc = ps_y.tile([P, share, width], F32, name="acc")
+                for t in range(first, first + share):
                     nc.tensor.matmul_mx(
-                        out=acc[:, e, :],
+                        out=acc[:, t - first, :],
                         lhsT=wd8_codes[:, t * P : (t + 1) * P].bitcast(FP8X4),
                         lhsT_scale=wd_scale[4:P, t * P : (t + 1) * P],
                         rhs=h_codes[c, 0][:].bitcast(FP8X4),
@@ -181,7 +201,7 @@ def tile_list_relu_mix_noneP_kernel(
                         stop=False,
                     )
                     nc.tensor.matmul_mx(
-                        out=acc[:, e, :],
+                        out=acc[:, t - first, :],
                         lhsT=wd4_codes[:, t * P : (t + 1) * P].bitcast(FP4X4),
                         lhsT_scale=wd_scale[:, t * P : (t + 1) * P],
                         rhs=h_codes[c, 1][:].bitcast(FP8X4),
@@ -189,88 +209,101 @@ def tile_list_relu_mix_noneP_kernel(
                         start=False,
                         stop=True,
                     )
-                nc.scalar.copy(out=y_sb[c][:, 2 * u : 2 * u + 2, :], in_=acc[:])
-            nc.sync.dma_start(out=y_rows[:, :, c * CH : (c + 1) * CH], in_=y_sb[c][:])
+                nc.scalar.copy(out=y_sb[c][:, first : first + share, :], in_=acc[:])
+            nc.sync.dma_start(out=y_rows[:, :, STARTS[c] : STARTS[c] + width], in_=y_sb[c][:])
 
         y_bf = {}
 
-        def weave_y(c):
-            y_bf[c] = keep.tile([P, CH * PACK], BF16, name="y_bf%d" % c, align_bytes=64)
-            nc.vector.tensor_copy(
+        def weave_y(c, copy):
+            y_bf[c] = keep.tile([P, WIDTHS[c] * PACK], BF16, name="y_bf%d" % c, align_bytes=64)
+            copy(
                 out=y_bf[c][:].rearrange("p (g e t) -> p g t e", e=4, t=PACK),
                 in_=y_sb[c][:].rearrange("p t (g e) -> p g t e", e=4),
             )
 
         def quant_y(c):
-            y_codes = keep.tile([P, CH], U32, name="y_codes%d" % c, align_bytes=64)
-            nc.vector.quantize_mx(
-                out=y_codes[:].bitcast(FP8X4), scales=y_scale[:, c * CH : (c + 1) * CH], in_=y_bf[c][:]
-            )
-            nc.sync.dma_start(out=y_words[:, c * CH : (c + 1) * CH], in_=y_codes[:].bitcast(I32))
+            cols = slice(STARTS[c], STARTS[c] + WIDTHS[c])
+            y_codes = keep.tile([P, WIDTHS[c]], U32, name="y_codes%d" % c, align_bytes=64)
+            nc.vector.quantize_mx(out=y_codes[:].bitcast(FP8X4), scales=y_scale[:, cols], in_=y_bf[c][:])
+            nc.sync.dma_start(out=y_words[:, cols], in_=y_codes[:].bitcast(I32))
 
+        on_vector, on_scalar = nc.vector.tensor_copy, nc.scalar.copy
+        for i in range(2):
+            for u in range(2):
+                gather_early(i, u)
         for c in range(NCH):
-            gather(0, c)
-        deal(nc.vector.tensor_copy, wu_scale[:], wu_sraw[:])
-        for i in range(1, PACK - 1):
-            for c in range(NCH):
-                gather(i, c)
-        gather(3, 0)
-        weave_x(0)
-        gather(3, 1)
-        weave_x(1)
+            weave_x(c, 0, on_scalar)
+        deal(on_vector, wu_scale[:], wu_sraw[:])
+        deal(on_scalar, wu_codes[0][:], wu_raw[0][:])
+        for c in range(NCH):
+            gather_late(2, c)
+        gather_late(3, 0)
+        weave_x(0, 1, on_scalar)
+        gather_late(3, 1)
+        weave_wg(0, 0, on_vector)
+        weave_wg(0, 1, on_scalar)
         quant_x(0)
-        gather(3, 2)
-        weave_wg(0, nc.vector.tensor_copy)
-        gather(3, 3)
         quant_wg(0)
-        deal(nc.vector.tensor_copy, wu_codes[:], wu_raw[:])
-        quant_x(1)
+        weave_x(1, 1, on_scalar)
+        gather_late(3, 2)
         up(0, 0, 0)
-        weave_x(2)
+        quant_x(1)
         up(0, 0, 1)
-        weave_wg(1, nc.scalar.copy)
+        weave_wg(1, 0, on_scalar)
+        gather_late(3, 3)
+        gather_late(3, 4)
+        deal(on_vector, wu_codes[1][:], wu_raw[1][:])
         up(1, 0, 0)
+        weave_wg(1, 1, on_scalar)
         quant_h(0, 0)
-        quant_wg(1)
         up(1, 0, 1)
-        deal(nc.scalar.copy, wd8_codes[:], wd8_raw[:])
-        deal(nc.scalar.copy, wd4_codes[:], wd4_raw[:])
-        wd_scale = keep.tile([P, N], U8, name="wd_scale", tag="x3", align_bytes=64)
-        deal(nc.vector.tensor_copy, wd_scale[:], wd_sraw[:])
+        quant_wg(1)
+        weave_x(2, 1, on_scalar)
         up(0, 1, 0)
         quant_h(1, 0)
-        quant_x(2)
+        deal(on_scalar, wd8_codes[:], wd8_raw[:])
         up(0, 1, 1)
-        weave_x(3)
+        quant_x(2)
+        deal(on_scalar, wd4_codes[:], wd4_raw[:])
+        deal(on_vector, wd_scale[:], wd_sraw[:])
         up(1, 1, 0)
         quant_h(0, 1)
-        quant_x(3)
+        weave_x(3, 1, on_scalar)
         up(1, 1, 1)
         down(0)
+        quant_x(3)
         up(2, 0, 0)
+        weave_x(4, 1, on_scalar)
         quant_h(1, 1)
         up(2, 0, 1)
         down(1)
-        weave_y(0)
+        weave_y(0, on_vector)
+        quant_x(4)
         up(2, 1, 0)
         quant_h(2, 0)
         quant_y(0)
         up(2, 1, 1)
-        weave_y(1)
+        weave_y(1, on_vector)
         up(3, 0, 0)
         quant_h(2, 1)
         quant_y(1)
-        up(3, 0, 1)
-        down(2)
         up(3, 1, 0)
+        down(2)
         quant_h(3, 0)
-        up(3, 1, 1)
-        weave_y(2)
+        up(4, 0, 0)
         quant_h(3, 1)
-        quant_y(2)
+        up(4, 1, 0)
         down(3)
-        weave_y(3)
+        quant_h(4, 0)
+        weave_y(2, on_vector)
+        quant_h(4, 1)
+        down(4)
+        quant_y(2)
+        weave_y(3, on_vector)
         quant_y(3)
+        weave_y(4, on_vector)
+        quant_y(4)
         y_sc = out_2[0].bitcast(I32)
         for q in range(4):
-            nc.sync.dma_start(out=y_sc[4 * q : 4 * q + 4, :], in_=y_scale[32 * q : 32 * q + 4, :].bitcast(I32))
+            queue = nc.scalar if q % 2 else nc.sync
+            queue.dma_start(out=y_sc[4 * q : 4 * q + 4, :], in_=y_scale[32 * q : 32 * q + 4, :].bitcast(I32))

@@ -43,44 +43,47 @@ def tile_list_relu_mix_noneP_kernel(
         x_rows = xT.rearrange("(p i) t -> p i t", i=PACK)
         x_sb = [keep.tile([P, T], F32, name="x_sb%d" % i) for i in range(PACK)]
         wg_rows = wg.rearrange("(p i) r -> p i r", i=PACK)
-        wg_raw = [[keep.tile([P, PACK, PASS // 2], F32, name="wg_raw%d_%d" % (b, u)) for u in range(2)] for b in range(2)]
+        wg_raw = [keep.tile([P, PACK, PASS], F32, name="wg_raw%d" % b) for b in range(2)]
         wu_raw = [keep.tile([P, PASS], U32, name="wu_raw%d" % b) for b in range(2)]
         wd8_raw = keep.tile([P, N], U32, name="wd8_raw")
         wd4_raw = keep.tile([P, N], U16, name="wd4_raw")
-        wu_sraw = keep.tile([P, PASS], U8, name="wu_sraw")
-        wd_sraw = keep.tile([P, N], U8, name="wd_sraw")
-        nc.vector.memset(wu_sraw[:].bitcast(I32), 0)
-        nc.vector.memset(wd_sraw[:].bitcast(I32), 0)
+        w_sraw = keep.tile([P, PASS], U8, name="w_sraw")
+        nc.vector.memset(w_sraw[:].bitcast(I32), 0)
 
-        def load_wg(b, u):
-            first = b * PASS + u * (PASS // 2)
-            nc.sync.dma_start(out=wg_raw[b][u][:], in_=wg_rows[:, :, first : first + PASS // 2])
+        def load_wg(b):
+            nc.sync.dma_start(out=wg_raw[b][:], in_=wg_rows[:, :, b * PASS : (b + 1) * PASS])
 
         wu_src = wu_words[0].rearrange("p r i -> p (r i)").bitcast(I32)
         wu_sc = wu_scales[0].bitcast(I32).rearrange("q (b w) -> b q w", b=2)
+        def load_wu_scales(q):
+            nc.sync.dma_start(out=w_sraw[32 * q + 4 : 32 * q + 12, :].bitcast(I32), in_=wu_sc[:, 4 * q : 4 * q + 4, :])
+
+        def load_wd8_scales(q):
+            nc.sync.dma_start(
+                out=w_sraw[32 * q + 12 : 32 * q + 16, :].bitcast(I32), in_=wd8_scales[0].bitcast(I32)[4 * q : 4 * q + 4, :]
+            )
+
         nc.sync.dma_start(offsets[:], offs)
         nc.sync.dma_start(out=wgt_sb[0][:], in_=wgt[:, 0:HALF])
         nc.sync.dma_start(out=x_sb[0][:], in_=x_rows[:, 0, :])
         nc.sync.dma_start(out=wgt_sb[1][:], in_=wgt[:, HALF:J])
         nc.sync.dma_start(out=x_sb[1][:], in_=x_rows[:, 1, :])
-        for q in range(4):
-            nc.sync.dma_start(out=wu_sraw[32 * q : 32 * q + 8, :].bitcast(I32), in_=wu_sc[:, 4 * q : 4 * q + 4, :])
+        for q in range(3):
+            load_wu_scales(q)
         nc.sync.dma_start(out=x_sb[2][:], in_=x_rows[:, 2, :])
+        load_wu_scales(3)
+        for q in range(4):
+            load_wd8_scales(q)
         nc.sync.dma_start(out=wu_raw[0][:].bitcast(I32), in_=wu_src[:, 0:PASS])
         nc.sync.dma_start(out=x_sb[3][:], in_=x_rows[:, 3, :])
-        load_wg(0, 0)
-        load_wg(0, 1)
+        load_wg(0)
         nc.sync.dma_start(out=wu_raw[1][:].bitcast(I32), in_=wu_src[:, PASS:R])
-        load_wg(1, 0)
-        load_wg(1, 1)
+        load_wg(1)
         nc.sync.dma_start(out=wd8_raw[:].bitcast(I32), in_=wd8_words[0].rearrange("p n i -> p (n i)").bitcast(I32))
         nc.sync.dma_start(out=wd4_raw[:].bitcast(I32), in_=wd4_words[0].bitcast(I32))
         for q in range(4):
-            nc.sync.dma_start(
-                out=wd_sraw[32 * q : 32 * q + 4, :].bitcast(I32), in_=wd4_scales[0].bitcast(I32)[4 * q : 4 * q + 4, :]
-            )
-            nc.sync.dma_start(
-                out=wd_sraw[32 * q + 4 : 32 * q + 8, :].bitcast(I32), in_=wd8_scales[0].bitcast(I32)[4 * q : 4 * q + 4, :]
+            nc.gpsimd.dma_start(
+                out=w_sraw[32 * q : 32 * q + 4, :].bitcast(I32), in_=wd4_scales[0].bitcast(I32)[4 * q : 4 * q + 4, :]
             )
 
         early = [keep.tile([P, 2, HALF], F32, name="early%d" % u) for u in range(2)]
@@ -107,8 +110,8 @@ def tile_list_relu_mix_noneP_kernel(
             first = STARTS[c] % HALF
             pair = late[c][:] if u else early[STARTS[c] // HALF][:, :, first : first + WIDTHS[c]]
             copy(
-                out=xg_bf[c][:].rearrange("p (j i) -> p j i", i=PACK)[:, :, 2 * u : 2 * u + 2],
-                in_=pair.rearrange("p i j -> p j i"),
+                out=xg_bf[c][:].rearrange("p (g e u i) -> p u g i e", e=2, u=2, i=2)[:, u],
+                in_=pair.rearrange("p i (g e) -> p g i e", e=2),
             )
 
         def quant_x(c):
@@ -118,22 +121,29 @@ def tile_list_relu_mix_noneP_kernel(
         wg_codes = [keep.tile([P, PASS], U32, name="wg_codes%d" % b, align_bytes=64) for b in range(2)]
         wg_scale = [keep.tile([P, PASS], U8, name="wg_scale%d" % b, align_bytes=64) for b in range(2)]
         wu_codes = [keep.tile([P, PASS], U32, name="wu_codes%d" % b, align_bytes=64) for b in range(2)]
-        wu_scale = keep.tile([P, PASS], U8, name="wu_scale", align_bytes=64)
+        w_scale = keep.tile([P, PASS], U8, name="w_scale", align_bytes=64)
         wd8_codes = keep.tile([P, N], U32, name="wd8_codes", align_bytes=64)
         wd4_codes = keep.tile([P, N], U16, name="wd4_codes", align_bytes=64)
-        wd_scale = keep.tile([P, N], U8, name="wd_scale", align_bytes=64)
 
         def weave_wg(b, u, copy):
             copy(
-                out=wg_bf[b][:].rearrange("p (t m i) -> p m i t", t=PACK, i=PACK)[:, u * (P // 2) : (u + 1) * (P // 2)],
-                in_=wg_raw[b][u][:].rearrange("p i (m t) -> p m i t", t=PACK),
+                out=wg_bf[b][:].rearrange("p (u t g e i) -> p u g e i t", u=2, t=2, e=2, i=PACK)[:, u],
+                in_=wg_raw[b][:].rearrange("p i (g e u t) -> p u g e i t", u=2, t=2, e=2)[:, u],
             )
 
-        def quant_wg(b):
-            nc.vector.quantize_mx(out=wg_codes[b][:].bitcast(FP8X4), scales=wg_scale[b][:], in_=wg_bf[b][:])
+        def quant_wg(b, u):
+            cols = slice(u * PASS // 2, (u + 1) * PASS // 2)
+            nc.vector.quantize_mx(
+                out=wg_codes[b][:, cols].bitcast(FP8X4),
+                scales=wg_scale[b][:, cols],
+                in_=wg_bf[b][:, u * PASS * 2 : (u + 1) * PASS * 2],
+            )
 
-        def deal(copy, dst, src):
-            copy(out=dst.rearrange("p (t m) -> p m t", t=PACK), in_=src.rearrange("p (m t) -> p m t", t=PACK))
+        def deal(copy, dst, src, run):
+            copy(
+                out=dst.rearrange("p (t g e) -> p g t e", t=PACK, e=run),
+                in_=src.rearrange("p (g e t) -> p g t e", t=PACK, e=run),
+            )
 
         h_bf = {}
         h_codes = {}
@@ -159,17 +169,17 @@ def tile_list_relu_mix_noneP_kernel(
                 nc.tensor.matmul_mx(
                     out=ub[:, t, :],
                     lhsT=wu_codes[b][:, t * P : (t + 1) * P].bitcast(FP8X4),
-                    lhsT_scale=wu_scale[4 * b : P, t * P : (t + 1) * P],
+                    lhsT_scale=w_scale[4 + 4 * b : P, t * P : (t + 1) * P],
                     rhs=xg_codes[c][:, cols].bitcast(FP8X4),
                     rhs_scale=xg_scale[c][:, cols],
                     start=True,
                     stop=True,
                 )
-            gate = ring.tile([P, SUB, PACK], F32, name="gate")
-            nc.scalar.activation(out=gate[:], in_=ga[:].rearrange("p t j -> p j t"), func=RELU)
+            gate = ring.tile([P, SUB // 2, PACK, 2], F32, name="gate")
+            nc.scalar.activation(out=gate[:], in_=ga[:].rearrange("p t (g e) -> p g t e", e=2), func=RELU)
             nc.vector.tensor_tensor(
-                h_bf[c, b][:, s * SUB * PACK : (s + 1) * SUB * PACK].rearrange("p (j t) -> p j t", t=PACK),
-                ub[:].rearrange("p t j -> p j t"),
+                h_bf[c, b][:, s * SUB * PACK : (s + 1) * SUB * PACK].rearrange("p (g e t) -> p g t e", e=2, t=PACK),
+                ub[:].rearrange("p t (g e) -> p g t e", e=2),
                 gate[:],
                 MULT,
             )
@@ -194,20 +204,21 @@ def tile_list_relu_mix_noneP_kernel(
                     nc.tensor.matmul_mx(
                         out=acc[:, t - first, :],
                         lhsT=wd8_codes[:, t * P : (t + 1) * P].bitcast(FP8X4),
-                        lhsT_scale=wd_scale[4:P, t * P : (t + 1) * P],
+                        lhsT_scale=w_scale[12:P, t * P : (t + 1) * P],
                         rhs=h_codes[c, 0][:].bitcast(FP8X4),
                         rhs_scale=h_scale[c, 0][:],
-                        start=True,
+                        start=t == first,
                         stop=False,
                     )
+                for t in range(first, first + share):
                     nc.tensor.matmul_mx(
                         out=acc[:, t - first, :],
                         lhsT=wd4_codes[:, t * P : (t + 1) * P].bitcast(FP4X4),
-                        lhsT_scale=wd_scale[:, t * P : (t + 1) * P],
+                        lhsT_scale=w_scale[:, t * P : (t + 1) * P],
                         rhs=h_codes[c, 1][:].bitcast(FP8X4),
                         rhs_scale=h_scale[c, 1][:],
                         start=False,
-                        stop=True,
+                        stop=t == first + share - 1,
                     )
                 nc.scalar.copy(out=y_sb[c][:, first : first + share, :], in_=acc[:])
             nc.sync.dma_start(out=y_rows[:, :, STARTS[c] : STARTS[c] + width], in_=y_sb[c][:])
@@ -217,8 +228,8 @@ def tile_list_relu_mix_noneP_kernel(
         def weave_y(c, copy):
             y_bf[c] = keep.tile([P, WIDTHS[c] * PACK], BF16, name="y_bf%d" % c, align_bytes=64)
             copy(
-                out=y_bf[c][:].rearrange("p (g e t) -> p g t e", e=4, t=PACK),
-                in_=y_sb[c][:].rearrange("p t (g e) -> p g t e", e=4),
+                out=y_bf[c][:].rearrange("p (g e t) -> p g t e", e=2, t=PACK),
+                in_=y_sb[c][:].rearrange("p t (g e) -> p g t e", e=2),
             )
 
         def quant_y(c):
@@ -233,76 +244,40 @@ def tile_list_relu_mix_noneP_kernel(
                 gather_early(i, u)
         for c in range(NCH):
             weave_x(c, 0, on_scalar)
-        deal(on_vector, wu_scale[:], wu_sraw[:])
-        deal(on_scalar, wu_codes[0][:], wu_raw[0][:])
+        deal(on_scalar, wu_codes[0][:], wu_raw[0][:], 4)
         for c in range(NCH):
             gather_late(2, c)
-        gather_late(3, 0)
+        deal(on_vector, w_scale[:], w_sraw[:], 16)
+        for c in range(NCH):
+            gather_late(3, c)
         weave_x(0, 1, on_scalar)
-        gather_late(3, 1)
         weave_wg(0, 0, on_vector)
         weave_wg(0, 1, on_scalar)
         quant_x(0)
-        quant_wg(0)
-        weave_x(1, 1, on_scalar)
-        gather_late(3, 2)
-        up(0, 0, 0)
-        quant_x(1)
-        up(0, 0, 1)
-        weave_wg(1, 0, on_scalar)
-        gather_late(3, 3)
-        gather_late(3, 4)
-        deal(on_vector, wu_codes[1][:], wu_raw[1][:])
-        up(1, 0, 0)
-        weave_wg(1, 1, on_scalar)
-        quant_h(0, 0)
-        up(1, 0, 1)
-        quant_wg(1)
-        weave_x(2, 1, on_scalar)
-        up(0, 1, 0)
-        quant_h(1, 0)
-        deal(on_scalar, wd8_codes[:], wd8_raw[:])
-        up(0, 1, 1)
-        quant_x(2)
-        deal(on_scalar, wd4_codes[:], wd4_raw[:])
-        deal(on_vector, wd_scale[:], wd_sraw[:])
-        up(1, 1, 0)
-        quant_h(0, 1)
-        weave_x(3, 1, on_scalar)
-        up(1, 1, 1)
-        down(0)
-        quant_x(3)
-        up(2, 0, 0)
-        weave_x(4, 1, on_scalar)
-        quant_h(1, 1)
-        up(2, 0, 1)
-        down(1)
-        weave_y(0, on_vector)
-        quant_x(4)
-        up(2, 1, 0)
-        quant_h(2, 0)
-        quant_y(0)
-        up(2, 1, 1)
-        weave_y(1, on_vector)
-        up(3, 0, 0)
-        quant_h(2, 1)
-        quant_y(1)
-        up(3, 1, 0)
-        down(2)
-        quant_h(3, 0)
-        up(4, 0, 0)
-        quant_h(3, 1)
-        up(4, 1, 0)
-        down(3)
-        quant_h(4, 0)
-        weave_y(2, on_vector)
-        quant_h(4, 1)
-        down(4)
-        quant_y(2)
-        weave_y(3, on_vector)
-        quant_y(3)
-        weave_y(4, on_vector)
-        quant_y(4)
+        quant_wg(0, 0)
+        quant_wg(0, 1)
+        for b in range(2):
+            for c in range(NCH):
+                if b == 0 and c + 1 < NCH:
+                    weave_x(c + 1, 1, on_scalar)
+                    quant_x(c + 1)
+                for s in range(WIDTHS[c] // SUB):
+                    up(c, b, s)
+                quant_h(c, b)
+                if b == 1:
+                    down(c)
+                if b == 0 and c == 1:
+                    deal(on_vector, wu_codes[1][:], wu_raw[1][:], 4)
+                    weave_wg(1, 0, on_vector)
+                    weave_wg(1, 1, on_scalar)
+                    quant_wg(1, 0)
+                    quant_wg(1, 1)
+                if b == 0 and c == 3:
+                    deal(on_scalar, wd8_codes[:], wd8_raw[:], 4)
+                    deal(on_scalar, wd4_codes[:], wd4_raw[:], 8)
+        for c in range(NCH):
+            weave_y(c, on_vector)
+            quant_y(c)
         y_sc = out_2[0].bitcast(I32)
         for q in range(4):
             queue = nc.scalar if q % 2 else nc.sync

@@ -25,6 +25,14 @@ HALF = J // 2
 WIDTHS = [256, 256, 256, 128, 128]
 STARTS = [sum(WIDTHS[:c]) for c in range(len(WIDTHS))]
 NCH = len(WIDTHS)
+QUARTER = J // 4
+X_PARTS = [(0, QUARTER), (QUARTER, QUARTER), (HALF, HALF)]
+H_PARTS = [[(0, HALF), (HALF, HALF)], list(zip(STARTS, WIDTHS))]
+
+
+def part_of(parts, col):
+    g = max(k for k, (first, width) in enumerate(parts) if first <= col)
+    return g, col - parts[g][0]
 
 
 def tile_list_relu_mix_noneP_kernel(
@@ -87,35 +95,30 @@ def tile_list_relu_mix_noneP_kernel(
             )
 
         early = [keep.tile([P, 2, HALF], F32, name="early%d" % u) for u in range(2)]
-        late = [keep.tile([P, 2, w], F32, name="late%d" % c) for c, w in enumerate(WIDTHS)]
-        xg_bf = [keep.tile([P, w * PACK], BF16, name="xg_bf%d" % c, align_bytes=64) for c, w in enumerate(WIDTHS)]
-        xg_codes = [keep.tile([P, w], U32, name="xg_codes%d" % c, align_bytes=64) for c, w in enumerate(WIDTHS)]
-        xg_scale = [keep.tile([P, w], U8, name="xg_scale%d" % c, align_bytes=64) for c, w in enumerate(WIDTHS)]
+        late = [keep.tile([P, 2, HALF], F32, name="late%d" % u) for u in range(2)]
+        xg_bf = [keep.tile([P, w * PACK], BF16, name="xg_bf%d" % g, align_bytes=64) for g, (f, w) in enumerate(X_PARTS)]
+        xg_codes = [keep.tile([P, w], U32, name="xg_codes%d" % g, align_bytes=64) for g, (f, w) in enumerate(X_PARTS)]
+        xg_scale = [keep.tile([P, w], U8, name="xg_scale%d" % g, align_bytes=64) for g, (f, w) in enumerate(X_PARTS)]
 
-        def gather(dst, i, first, width):
+        def gather(i, first, width):
+            u, at = divmod(first, HALF)
             nc.vector.tensor_tensor(
-                dst,
+                (early, late)[i // 2][u][:, i % 2, at : at + width],
                 x_sb[i][:].indirect(offsets[:, first // 16 : (first + width) // 16]),
-                wgt_sb[first // HALF][:, first % HALF : first % HALF + width],
+                wgt_sb[u][:, at : at + width],
                 MULT,
             )
 
-        def gather_early(i, u):
-            gather(early[u][:, i, :], i, u * HALF, HALF)
-
-        def gather_late(i, c):
-            gather(late[c][:, i - 2, :], i, STARTS[c], WIDTHS[c])
-
-        def weave_x(c, u, copy):
-            first = STARTS[c] % HALF
-            pair = late[c][:] if u else early[STARTS[c] // HALF][:, :, first : first + WIDTHS[c]]
-            copy(
-                out=xg_bf[c][:].rearrange("p (g e u i) -> p u g i e", e=2, u=2, i=2)[:, u],
-                in_=pair.rearrange("p i (g e) -> p g i e", e=2),
+        def weave_x(pair, first):
+            u, at = divmod(first, HALF)
+            g, to = part_of(X_PARTS, first)
+            nc.scalar.copy(
+                out=xg_bf[g][:, to * PACK : (to + QUARTER) * PACK].rearrange("p (g e u i) -> p u g i e", e=2, u=2, i=2)[:, pair],
+                in_=(early, late)[pair][u][:, :, at : at + QUARTER].rearrange("p i (g e) -> p g i e", e=2),
             )
 
-        def quant_x(c):
-            nc.vector.quantize_mx(out=xg_codes[c][:].bitcast(FP8X4), scales=xg_scale[c][:], in_=xg_bf[c][:])
+        def quant_x(g):
+            nc.vector.quantize_mx(out=xg_codes[g][:].bitcast(FP8X4), scales=xg_scale[g][:], in_=xg_bf[g][:])
 
         wg_bf = [keep.tile([P, PASS * PACK], BF16, name="wg_bf%d" % b, align_bytes=64) for b in range(2)]
         wg_codes = [keep.tile([P, PASS], U32, name="wg_codes%d" % b, align_bytes=64) for b in range(2)]
@@ -131,12 +134,12 @@ def tile_list_relu_mix_noneP_kernel(
                 in_=wg_raw[b][:].rearrange("p i (g e u t) -> p u g e i t", u=2, t=2, e=2)[:, u],
             )
 
-        def quant_wg(b, u):
-            cols = slice(u * PASS // 2, (u + 1) * PASS // 2)
+        def quant_wg(b, first, width):
+            cols = slice(first, first + width)
             nc.vector.quantize_mx(
                 out=wg_codes[b][:, cols].bitcast(FP8X4),
                 scales=wg_scale[b][:, cols],
-                in_=wg_bf[b][:, u * PASS * 2 : (u + 1) * PASS * 2],
+                in_=wg_bf[b][:, first * PACK : (first + width) * PACK],
             )
 
         def deal(copy, dst, src, run):
@@ -145,14 +148,14 @@ def tile_list_relu_mix_noneP_kernel(
                 in_=src.rearrange("p (g e t) -> p g t e", t=PACK, e=run),
             )
 
-        h_bf = {}
-        h_codes = {}
-        h_scale = {}
+        h_bf = [[keep.tile([P, w * PACK], BF16, name="h_bf%d_%d" % (b, g), align_bytes=64) for g, (f, w) in enumerate(H_PARTS[b])] for b in range(2)]
+        h_codes = [[keep.tile([P, w], U32, name="h_codes%d_%d" % (b, g), align_bytes=64) for g, (f, w) in enumerate(H_PARTS[b])] for b in range(2)]
+        h_scale = [[keep.tile([P, w], U8, name="h_scale%d_%d" % (b, g), align_bytes=64) for g, (f, w) in enumerate(H_PARTS[b])] for b in range(2)]
 
-        def up(c, b, s):
-            if s == 0:
-                h_bf[c, b] = keep.tile([P, WIDTHS[c] * PACK], BF16, name="h_bf%d_%d" % (c, b), align_bytes=64)
-            cols = slice(s * SUB, (s + 1) * SUB)
+        def up(b, first):
+            gx, at = part_of(X_PARTS, first)
+            gh, to = part_of(H_PARTS[b], first)
+            cols = slice(at, at + SUB)
             ga = ps_ga.tile([P, PACK, SUB], F32, name="ga")
             ub = ps_ub.tile([P, PACK, SUB], F32, name="ub")
             for t in range(PACK):
@@ -160,8 +163,8 @@ def tile_list_relu_mix_noneP_kernel(
                     out=ga[:, t, :],
                     lhsT=wg_codes[b][:, t * P : (t + 1) * P].bitcast(FP8X4),
                     lhsT_scale=wg_scale[b][:, t * P : (t + 1) * P],
-                    rhs=xg_codes[c][:, cols].bitcast(FP8X4),
-                    rhs_scale=xg_scale[c][:, cols],
+                    rhs=xg_codes[gx][:, cols].bitcast(FP8X4),
+                    rhs_scale=xg_scale[gx][:, cols],
                     start=True,
                     stop=True,
                 )
@@ -170,24 +173,22 @@ def tile_list_relu_mix_noneP_kernel(
                     out=ub[:, t, :],
                     lhsT=wu_codes[b][:, t * P : (t + 1) * P].bitcast(FP8X4),
                     lhsT_scale=w_scale[4 + 4 * b : P, t * P : (t + 1) * P],
-                    rhs=xg_codes[c][:, cols].bitcast(FP8X4),
-                    rhs_scale=xg_scale[c][:, cols],
+                    rhs=xg_codes[gx][:, cols].bitcast(FP8X4),
+                    rhs_scale=xg_scale[gx][:, cols],
                     start=True,
                     stop=True,
                 )
             gate = ring.tile([P, SUB // 2, PACK, 2], F32, name="gate")
             nc.scalar.activation(out=gate[:], in_=ga[:].rearrange("p t (g e) -> p g t e", e=2), func=RELU)
             nc.vector.tensor_tensor(
-                h_bf[c, b][:, s * SUB * PACK : (s + 1) * SUB * PACK].rearrange("p (g e t) -> p g t e", e=2, t=PACK),
+                h_bf[b][gh][:, to * PACK : (to + SUB) * PACK].rearrange("p (g e t) -> p g t e", e=2, t=PACK),
                 ub[:].rearrange("p t (g e) -> p g t e", e=2),
                 gate[:],
                 MULT,
             )
 
-        def quant_h(c, b):
-            h_codes[c, b] = keep.tile([P, WIDTHS[c]], U32, name="h_codes%d_%d" % (c, b), align_bytes=64)
-            h_scale[c, b] = keep.tile([P, WIDTHS[c]], U8, name="h_scale%d_%d" % (c, b), align_bytes=64)
-            nc.vector.quantize_mx(out=h_codes[c, b][:].bitcast(FP8X4), scales=h_scale[c, b][:], in_=h_bf[c, b][:])
+        def quant_h(b, g):
+            nc.vector.quantize_mx(out=h_codes[b][g][:].bitcast(FP8X4), scales=h_scale[b][g][:], in_=h_bf[b][g][:])
 
         y_rows = out_0.rearrange("(p t) j -> p t j", t=PACK)
         y_words = out_1[0].rearrange("p j i -> p (j i)").bitcast(I32)
@@ -197,6 +198,7 @@ def tile_list_relu_mix_noneP_kernel(
         def down(c):
             width = WIDTHS[c]
             share = BANK // width
+            g0, at = part_of(H_PARTS[0], STARTS[c])
             y_sb[c] = keep.tile([P, PACK, width], F32, name="y_sb%d" % c)
             for first in range(0, PACK, share):
                 acc = ps_y.tile([P, share, width], F32, name="acc")
@@ -205,8 +207,8 @@ def tile_list_relu_mix_noneP_kernel(
                         out=acc[:, t - first, :],
                         lhsT=wd8_codes[:, t * P : (t + 1) * P].bitcast(FP8X4),
                         lhsT_scale=w_scale[12:P, t * P : (t + 1) * P],
-                        rhs=h_codes[c, 0][:].bitcast(FP8X4),
-                        rhs_scale=h_scale[c, 0][:],
+                        rhs=h_codes[0][g0][:, at : at + width].bitcast(FP8X4),
+                        rhs_scale=h_scale[0][g0][:, at : at + width],
                         start=t == first,
                         stop=False,
                     )
@@ -215,8 +217,8 @@ def tile_list_relu_mix_noneP_kernel(
                         out=acc[:, t - first, :],
                         lhsT=wd4_codes[:, t * P : (t + 1) * P].bitcast(FP4X4),
                         lhsT_scale=w_scale[:, t * P : (t + 1) * P],
-                        rhs=h_codes[c, 1][:].bitcast(FP8X4),
-                        rhs_scale=h_scale[c, 1][:],
+                        rhs=h_codes[1][c][:].bitcast(FP8X4),
+                        rhs_scale=h_scale[1][c][:],
                         start=False,
                         stop=t == first + share - 1,
                     )
@@ -240,44 +242,58 @@ def tile_list_relu_mix_noneP_kernel(
 
         on_vector, on_scalar = nc.vector.tensor_copy, nc.scalar.copy
         for i in range(2):
-            for u in range(2):
-                gather_early(i, u)
-        for c in range(NCH):
-            weave_x(c, 0, on_scalar)
+            for first in (0, HALF):
+                gather(i, first, HALF)
+        for first in range(0, J, QUARTER):
+            weave_x(0, first)
         deal(on_scalar, wu_codes[0][:], wu_raw[0][:], 4)
-        for c in range(NCH):
-            gather_late(2, c)
+        for first in (0, HALF):
+            gather(2, first, HALF)
         deal(on_vector, w_scale[:], w_sraw[:], 16)
-        for c in range(NCH):
-            gather_late(3, c)
-        weave_x(0, 1, on_scalar)
+        for first, width in X_PARTS:
+            gather(3, first, width)
+        weave_x(1, 0)
         weave_wg(0, 0, on_vector)
         weave_wg(0, 1, on_scalar)
         quant_x(0)
-        quant_wg(0, 0)
-        quant_wg(0, 1)
-        for b in range(2):
-            for c in range(NCH):
-                if b == 0 and c + 1 < NCH:
-                    weave_x(c + 1, 1, on_scalar)
-                    quant_x(c + 1)
-                for s in range(WIDTHS[c] // SUB):
-                    up(c, b, s)
-                quant_h(c, b)
-                if b == 1:
-                    down(c)
-                if b == 0 and c == 1:
-                    deal(on_vector, wu_codes[1][:], wu_raw[1][:], 4)
-                    weave_wg(1, 0, on_vector)
-                    weave_wg(1, 1, on_scalar)
-                    quant_wg(1, 0)
-                    quant_wg(1, 1)
-                if b == 0 and c == 3:
-                    deal(on_scalar, wd8_codes[:], wd8_raw[:], 4)
-                    deal(on_scalar, wd4_codes[:], wd4_raw[:], 8)
+        quant_wg(0, 0, PASS // 2)
+        quant_wg(0, PASS // 2, PASS // 2)
+        weave_x(1, QUARTER)
+        up(0, 0)
+        quant_x(1)
+        up(0, SUB)
+        weave_x(1, HALF)
+        up(0, 2 * SUB)
+        weave_x(1, HALF + QUARTER)
+        up(0, 3 * SUB)
+        quant_x(2)
+        weave_wg(1, 0, on_vector)
+        up(0, 4 * SUB)
+        weave_wg(1, 1, on_scalar)
+        quant_h(0, 0)
+        up(0, 5 * SUB)
+        deal(on_scalar, wu_codes[1][:], wu_raw[1][:], 4)
+        quant_wg(1, 0, PASS)
+        up(0, 6 * SUB)
+        deal(on_scalar, wd8_codes[:], wd8_raw[:], 4)
+        up(0, 7 * SUB)
+        deal(on_scalar, wd4_codes[:], wd4_raw[:], 8)
         for c in range(NCH):
+            for first in range(STARTS[c], STARTS[c] + WIDTHS[c], SUB):
+                up(1, first)
+                if first == STARTS[c]:
+                    if c == 0:
+                        quant_h(0, 1)
+                    else:
+                        quant_h(1, c - 1)
+                        down(c - 1)
+        quant_h(1, NCH - 1)
+        down(NCH - 1)
+        weave_y(0, on_scalar)
+        for c in range(1, NCH):
             weave_y(c, on_vector)
-            quant_y(c)
+            quant_y(c - 1)
+        quant_y(NCH - 1)
         y_sc = out_2[0].bitcast(I32)
         for q in range(4):
             queue = nc.scalar if q % 2 else nc.sync

@@ -20,14 +20,17 @@ P = 128
 PACK = 4
 PASS = P * PACK
 BANK = 512
-SUB = 128
+LINE = 16
+LIST_ROWS = 16
+SUB = BANK // PACK
 HALF = J // 2
-WIDTHS = [256, 256, 256, 128, 128]
-STARTS = [sum(WIDTHS[:c]) for c in range(len(WIDTHS))]
-NCH = len(WIDTHS)
 QUARTER = J // 4
+
 X_PARTS = [(0, QUARTER), (QUARTER, QUARTER), (HALF, HALF)]
-H_PARTS = [[(0, HALF), (HALF, HALF)], list(zip(STARTS, WIDTHS))]
+Y_PARTS = [(0, QUARTER), (QUARTER, QUARTER), (HALF, QUARTER), (J - 2 * SUB, SUB), (J - SUB, SUB)]
+H_PARTS = [[(0, HALF), (HALF, HALF)], Y_PARTS]
+
+WD4_ROW, WU_ROWS, WD8_ROW = 0, (4, 8), 12
 
 
 def part_of(parts, col):
@@ -39,14 +42,21 @@ def tile_list_relu_mix_noneP_kernel(
     tc, xT, wgt, wg, wu_words, wu_scales, wd8_words, wd8_scales, wd4_words, wd4_scales, offs, out_0, out_1, out_2
 ):
     nc = tc.nc
+    on_vector, on_scalar = nc.vector.tensor_copy, nc.scalar.copy
     with ExitStack() as ctx:
         keep = ctx.enter_context(tc.tile_pool(name="keep", bufs=1))
         ring = ctx.enter_context(tc.tile_pool(name="ring", bufs=3))
-        ps_ga = ctx.enter_context(tc.psum_pool(name="ps_ga", bufs=2))
+        ps_ga = ctx.enter_context(tc.psum_pool(name="ps_ga", bufs=3))
         ps_ub = ctx.enter_context(tc.psum_pool(name="ps_ub", bufs=3))
-        ps_y = ctx.enter_context(tc.psum_pool(name="ps_y", bufs=3))
+        ps_y = ctx.enter_context(tc.psum_pool(name="ps_y", bufs=2))
 
-        offsets = keep.tile([P, J // 16], U16, name="offsets")
+        def part_tiles(name, parts, dtype, per_column=1):
+            return [
+                keep.tile([P, width * per_column], dtype, name="%s%d" % (name, g), align_bytes=64)
+                for g, (first, width) in enumerate(parts)
+            ]
+
+        offsets = keep.tile([P, J // LIST_ROWS], U16, name="offsets")
         wgt_sb = [keep.tile([P, HALF], F32, name="wgt_sb%d" % u) for u in range(2)]
         x_rows = xT.rearrange("(p i) t -> p i t", i=PACK)
         x_sb = [keep.tile([P, T], F32, name="x_sb%d" % i) for i in range(PACK)]
@@ -55,56 +65,63 @@ def tile_list_relu_mix_noneP_kernel(
         wu_raw = [keep.tile([P, PASS], U32, name="wu_raw%d" % b) for b in range(2)]
         wd8_raw = keep.tile([P, N], U32, name="wd8_raw")
         wd4_raw = keep.tile([P, N], U16, name="wd4_raw")
-        w_sraw = keep.tile([P, PASS], U8, name="w_sraw")
-        nc.vector.memset(w_sraw[:].bitcast(I32), 0)
+        w_scale_raw = keep.tile([P, PASS], U8, name="w_scale_raw")
+        nc.vector.memset(w_scale_raw[:].bitcast(I32), 0)
+
+        wu_src = wu_words[0].rearrange("p r i -> p (r i)").bitcast(I32)
+        wu_scale_src = wu_scales[0].bitcast(I32).rearrange("q (b w) -> b q w", b=2)
+
+        def load_x(i):
+            nc.sync.dma_start(out=x_sb[i][:], in_=x_rows[:, i, :])
+
+        def load_wgt(u):
+            nc.sync.dma_start(out=wgt_sb[u][:], in_=wgt[:, u * HALF : (u + 1) * HALF])
 
         def load_wg(b):
             nc.sync.dma_start(out=wg_raw[b][:], in_=wg_rows[:, :, b * PASS : (b + 1) * PASS])
 
-        wu_src = wu_words[0].rearrange("p r i -> p (r i)").bitcast(I32)
-        wu_sc = wu_scales[0].bitcast(I32).rearrange("q (b w) -> b q w", b=2)
-        def load_wu_scales(q):
-            nc.sync.dma_start(out=w_sraw[32 * q + 4 : 32 * q + 12, :].bitcast(I32), in_=wu_sc[:, 4 * q : 4 * q + 4, :])
+        def load_wu(b):
+            nc.sync.dma_start(out=wu_raw[b][:].bitcast(I32), in_=wu_src[:, b * PASS : (b + 1) * PASS])
 
-        def load_wd8_scales(q):
-            nc.sync.dma_start(
-                out=w_sraw[32 * q + 12 : 32 * q + 16, :].bitcast(I32), in_=wd8_scales[0].bitcast(I32)[4 * q : 4 * q + 4, :]
-            )
+        def load_wu_scales(q):
+            first = 32 * q + WU_ROWS[0]
+            nc.sync.dma_start(out=w_scale_raw[first : first + 8, :].bitcast(I32), in_=wu_scale_src[:, 4 * q : 4 * q + 4, :])
+
+        def load_wd_scales(queue, scales, row, q):
+            first = 32 * q + row
+            queue.dma_start(out=w_scale_raw[first : first + 4, :].bitcast(I32), in_=scales[0].bitcast(I32)[4 * q : 4 * q + 4, :])
 
         nc.sync.dma_start(offsets[:], offs)
-        nc.sync.dma_start(out=wgt_sb[0][:], in_=wgt[:, 0:HALF])
-        nc.sync.dma_start(out=x_sb[0][:], in_=x_rows[:, 0, :])
-        nc.sync.dma_start(out=wgt_sb[1][:], in_=wgt[:, HALF:J])
-        nc.sync.dma_start(out=x_sb[1][:], in_=x_rows[:, 1, :])
+        load_wgt(0)
+        load_x(0)
+        load_wgt(1)
+        load_x(1)
         for q in range(3):
             load_wu_scales(q)
-        nc.sync.dma_start(out=x_sb[2][:], in_=x_rows[:, 2, :])
+        load_x(2)
         load_wu_scales(3)
         for q in range(4):
-            load_wd8_scales(q)
-        nc.sync.dma_start(out=wu_raw[0][:].bitcast(I32), in_=wu_src[:, 0:PASS])
-        nc.sync.dma_start(out=x_sb[3][:], in_=x_rows[:, 3, :])
+            load_wd_scales(nc.sync, wd8_scales, WD8_ROW, q)
+        load_wu(0)
+        load_x(3)
         load_wg(0)
-        nc.sync.dma_start(out=wu_raw[1][:].bitcast(I32), in_=wu_src[:, PASS:R])
+        load_wu(1)
         load_wg(1)
         nc.sync.dma_start(out=wd8_raw[:].bitcast(I32), in_=wd8_words[0].rearrange("p n i -> p (n i)").bitcast(I32))
         nc.sync.dma_start(out=wd4_raw[:].bitcast(I32), in_=wd4_words[0].bitcast(I32))
         for q in range(4):
-            nc.gpsimd.dma_start(
-                out=w_sraw[32 * q : 32 * q + 4, :].bitcast(I32), in_=wd4_scales[0].bitcast(I32)[4 * q : 4 * q + 4, :]
-            )
+            load_wd_scales(nc.gpsimd, wd4_scales, WD4_ROW, q)
 
-        early = [keep.tile([P, 2, HALF], F32, name="early%d" % u) for u in range(2)]
-        late = [keep.tile([P, 2, HALF], F32, name="late%d" % u) for u in range(2)]
-        xg_bf = [keep.tile([P, w * PACK], BF16, name="xg_bf%d" % g, align_bytes=64) for g, (f, w) in enumerate(X_PARTS)]
-        xg_codes = [keep.tile([P, w], U32, name="xg_codes%d" % g, align_bytes=64) for g, (f, w) in enumerate(X_PARTS)]
-        xg_scale = [keep.tile([P, w], U8, name="xg_scale%d" % g, align_bytes=64) for g, (f, w) in enumerate(X_PARTS)]
+        picked = [[keep.tile([P, 2, HALF], F32, name="picked%d_%d" % (pair, u)) for u in range(2)] for pair in range(2)]
+        xg_bf = part_tiles("xg_bf", X_PARTS, BF16, PACK)
+        xg_codes = part_tiles("xg_codes", X_PARTS, U32)
+        xg_scale = part_tiles("xg_scale", X_PARTS, U8)
 
         def gather(i, first, width):
             u, at = divmod(first, HALF)
             nc.vector.tensor_tensor(
-                (early, late)[i // 2][u][:, i % 2, at : at + width],
-                x_sb[i][:].indirect(offsets[:, first // 16 : (first + width) // 16]),
+                picked[i // 2][u][:, i % 2, at : at + width],
+                x_sb[i][:].indirect(offsets[:, first // LIST_ROWS : (first + width) // LIST_ROWS]),
                 wgt_sb[u][:, at : at + width],
                 MULT,
             )
@@ -114,7 +131,7 @@ def tile_list_relu_mix_noneP_kernel(
             g, to = part_of(X_PARTS, first)
             nc.scalar.copy(
                 out=xg_bf[g][:, to * PACK : (to + QUARTER) * PACK].rearrange("p (g e u i) -> p u g i e", e=2, u=2, i=2)[:, pair],
-                in_=(early, late)[pair][u][:, :, at : at + QUARTER].rearrange("p i (g e) -> p g i e", e=2),
+                in_=picked[pair][u][:, :, at : at + QUARTER].rearrange("p i (g e) -> p g i e", e=2),
             )
 
         def quant_x(g):
@@ -142,116 +159,142 @@ def tile_list_relu_mix_noneP_kernel(
                 in_=wg_bf[b][:, first * PACK : (first + width) * PACK],
             )
 
-        def deal(copy, dst, src, run):
+        def deal(copy, dst, src, element_bytes):
+            run = LINE // element_bytes
             copy(
-                out=dst.rearrange("p (t g e) -> p g t e", t=PACK, e=run),
-                in_=src.rearrange("p (g e t) -> p g t e", t=PACK, e=run),
+                out=dst[:].rearrange("p (t g e) -> p g t e", t=PACK, e=run),
+                in_=src[:].rearrange("p (g e t) -> p g t e", t=PACK, e=run),
             )
 
-        h_bf = [[keep.tile([P, w * PACK], BF16, name="h_bf%d_%d" % (b, g), align_bytes=64) for g, (f, w) in enumerate(H_PARTS[b])] for b in range(2)]
-        h_codes = [[keep.tile([P, w], U32, name="h_codes%d_%d" % (b, g), align_bytes=64) for g, (f, w) in enumerate(H_PARTS[b])] for b in range(2)]
-        h_scale = [[keep.tile([P, w], U8, name="h_scale%d_%d" % (b, g), align_bytes=64) for g, (f, w) in enumerate(H_PARTS[b])] for b in range(2)]
+        h_bf = [part_tiles("h_bf%d_" % b, H_PARTS[b], BF16, PACK) for b in range(2)]
+        h_codes = [part_tiles("h_codes%d_" % b, H_PARTS[b], U32) for b in range(2)]
+        h_scale = [part_tiles("h_scale%d_" % b, H_PARTS[b], U8) for b in range(2)]
+        gate = {}
 
-        def up(b, first):
+        def make_gate(b, first):
+            gx, at = part_of(X_PARTS, first)
+            cols = slice(at, at + QUARTER)
+            gate[b, first] = ring.tile([P, PACK, QUARTER], F32, name="gate")
+            for u in range(2):
+                ga = ps_ga.tile([P, 2, QUARTER], F32, name="ga")
+                for e in range(2):
+                    t = 2 * u + e
+                    nc.tensor.matmul_mx(
+                        out=ga[:, e, :],
+                        lhsT=wg_codes[b][:, t * P : (t + 1) * P].bitcast(FP8X4),
+                        lhsT_scale=wg_scale[b][:, t * P : (t + 1) * P],
+                        rhs=xg_codes[gx][:, cols].bitcast(FP8X4),
+                        rhs_scale=xg_scale[gx][:, cols],
+                        start=True,
+                        stop=True,
+                    )
+                nc.scalar.activation(out=gate[b, first][:, 2 * u : 2 * u + 2, :], in_=ga[:], func=RELU)
+
+        def make_h(b, first):
             gx, at = part_of(X_PARTS, first)
             gh, to = part_of(H_PARTS[b], first)
             cols = slice(at, at + SUB)
-            ga = ps_ga.tile([P, PACK, SUB], F32, name="ga")
             ub = ps_ub.tile([P, PACK, SUB], F32, name="ub")
-            for t in range(PACK):
-                nc.tensor.matmul_mx(
-                    out=ga[:, t, :],
-                    lhsT=wg_codes[b][:, t * P : (t + 1) * P].bitcast(FP8X4),
-                    lhsT_scale=wg_scale[b][:, t * P : (t + 1) * P],
-                    rhs=xg_codes[gx][:, cols].bitcast(FP8X4),
-                    rhs_scale=xg_scale[gx][:, cols],
-                    start=True,
-                    stop=True,
-                )
             for t in range(PACK):
                 nc.tensor.matmul_mx(
                     out=ub[:, t, :],
                     lhsT=wu_codes[b][:, t * P : (t + 1) * P].bitcast(FP8X4),
-                    lhsT_scale=w_scale[4 + 4 * b : P, t * P : (t + 1) * P],
+                    lhsT_scale=w_scale[WU_ROWS[b] : P, t * P : (t + 1) * P],
                     rhs=xg_codes[gx][:, cols].bitcast(FP8X4),
                     rhs_scale=xg_scale[gx][:, cols],
                     start=True,
                     stop=True,
                 )
-            gate = ring.tile([P, SUB // 2, PACK, 2], F32, name="gate")
-            nc.scalar.activation(out=gate[:], in_=ga[:].rearrange("p t (g e) -> p g t e", e=2), func=RELU)
+            off = first % QUARTER
             nc.vector.tensor_tensor(
-                h_bf[b][gh][:, to * PACK : (to + SUB) * PACK].rearrange("p (g e t) -> p g t e", e=2, t=PACK),
-                ub[:].rearrange("p t (g e) -> p g t e", e=2),
-                gate[:],
+                h_bf[b][gh][:, to * PACK : (to + SUB) * PACK].rearrange("p (g e t) -> p g t e", e=4, t=PACK),
+                ub[:].rearrange("p t (g e) -> p g t e", e=4),
+                gate[b, first - off][:, :, off : off + SUB].rearrange("p t (g e) -> p g t e", e=4),
                 MULT,
             )
-
-        def quant_h(b, g):
-            nc.vector.quantize_mx(out=h_codes[b][g][:].bitcast(FP8X4), scales=h_scale[b][g][:], in_=h_bf[b][g][:])
 
         y_rows = out_0.rearrange("(p t) j -> p t j", t=PACK)
         y_words = out_1[0].rearrange("p j i -> p (j i)").bitcast(I32)
         y_scale = keep.tile([P, J], U8, name="y_scale", align_bytes=64)
-        y_sb = {}
+        y_codes = keep.tile([P, J], U32, name="y_codes", align_bytes=64)
+        y_sb = [keep.tile([P, PACK, width], F32, name="y_sb%d" % c) for c, (first, width) in enumerate(Y_PARTS)]
+        y_bf = part_tiles("y_bf", Y_PARTS, BF16, PACK)
 
-        def down(c):
-            width = WIDTHS[c]
-            share = BANK // width
-            g0, at = part_of(H_PARTS[0], STARTS[c])
-            y_sb[c] = keep.tile([P, PACK, width], F32, name="y_sb%d" % c)
-            for first in range(0, PACK, share):
-                acc = ps_y.tile([P, share, width], F32, name="acc")
-                for t in range(first, first + share):
+        def make_y(c):
+            first, width = Y_PARTS[c]
+            per_bank = BANK // width
+            g0, at = part_of(H_PARTS[0], first)
+            for t0 in range(0, PACK, per_bank):
+                acc = ps_y.tile([P, per_bank, width], F32, name="acc")
+                for t in range(t0, t0 + per_bank):
                     nc.tensor.matmul_mx(
-                        out=acc[:, t - first, :],
+                        out=acc[:, t - t0, :],
                         lhsT=wd8_codes[:, t * P : (t + 1) * P].bitcast(FP8X4),
-                        lhsT_scale=w_scale[12:P, t * P : (t + 1) * P],
+                        lhsT_scale=w_scale[WD8_ROW:P, t * P : (t + 1) * P],
                         rhs=h_codes[0][g0][:, at : at + width].bitcast(FP8X4),
                         rhs_scale=h_scale[0][g0][:, at : at + width],
-                        start=t == first,
+                        start=t == t0,
                         stop=False,
                     )
-                for t in range(first, first + share):
+                for t in range(t0, t0 + per_bank):
                     nc.tensor.matmul_mx(
-                        out=acc[:, t - first, :],
+                        out=acc[:, t - t0, :],
                         lhsT=wd4_codes[:, t * P : (t + 1) * P].bitcast(FP4X4),
-                        lhsT_scale=w_scale[:, t * P : (t + 1) * P],
+                        lhsT_scale=w_scale[WD4_ROW:P, t * P : (t + 1) * P],
                         rhs=h_codes[1][c][:].bitcast(FP8X4),
                         rhs_scale=h_scale[1][c][:],
                         start=False,
-                        stop=t == first + share - 1,
+                        stop=t == t0 + per_bank - 1,
                     )
-                nc.scalar.copy(out=y_sb[c][:, first : first + share, :], in_=acc[:])
-            nc.sync.dma_start(out=y_rows[:, :, STARTS[c] : STARTS[c] + width], in_=y_sb[c][:])
+                nc.scalar.copy(out=y_sb[c][:, t0 : t0 + per_bank, :], in_=acc[:])
+            nc.sync.dma_start(out=y_rows[:, :, first : first + width], in_=y_sb[c][:])
 
-        y_bf = {}
+        def finish_h(b, first):
+            g, to = part_of(H_PARTS[b], first)
+            if to + SUB == H_PARTS[b][g][1]:
+                nc.vector.quantize_mx(out=h_codes[b][g][:].bitcast(FP8X4), scales=h_scale[b][g][:], in_=h_bf[b][g][:])
+                if b == 1:
+                    make_y(g)
 
         def weave_y(c, copy):
-            y_bf[c] = keep.tile([P, WIDTHS[c] * PACK], BF16, name="y_bf%d" % c, align_bytes=64)
             copy(
                 out=y_bf[c][:].rearrange("p (g e t) -> p g t e", e=2, t=PACK),
                 in_=y_sb[c][:].rearrange("p t (g e) -> p g t e", e=2),
             )
 
         def quant_y(c):
-            cols = slice(STARTS[c], STARTS[c] + WIDTHS[c])
-            y_codes = keep.tile([P, WIDTHS[c]], U32, name="y_codes%d" % c, align_bytes=64)
-            nc.vector.quantize_mx(out=y_codes[:].bitcast(FP8X4), scales=y_scale[:, cols], in_=y_bf[c][:])
-            nc.sync.dma_start(out=y_words[:, cols], in_=y_codes[:].bitcast(I32))
+            first, width = Y_PARTS[c]
+            cols = slice(first, first + width)
+            nc.vector.quantize_mx(out=y_codes[:, cols].bitcast(FP8X4), scales=y_scale[:, cols], in_=y_bf[c][:])
+            if cols.stop % HALF == 0:
+                half = slice(cols.stop - HALF, cols.stop)
+                nc.sync.dma_start(out=y_words[:, half], in_=y_codes[:, half].bitcast(I32))
 
-        on_vector, on_scalar = nc.vector.tensor_copy, nc.scalar.copy
+        def prepare_upper_first_stage():
+            weave_wg(1, 0, on_vector)
+            weave_wg(1, 1, on_scalar)
+            weave_x(1, HALF)
+            weave_x(1, HALF + QUARTER)
+            quant_x(2)
+            quant_wg(1, 0, PASS)
+            deal(on_scalar, wu_codes[1], wu_raw[1], 4)
+
+        def prepare_second_stage():
+            deal(on_scalar, wd8_codes, wd8_raw, 4)
+            deal(on_scalar, wd4_codes, wd4_raw, 2)
+
         for i in range(2):
             for first in (0, HALF):
                 gather(i, first, HALF)
         for first in range(0, J, QUARTER):
             weave_x(0, first)
-        deal(on_scalar, wu_codes[0][:], wu_raw[0][:], 4)
+        deal(on_scalar, wu_codes[0], wu_raw[0], 4)
         for first in (0, HALF):
             gather(2, first, HALF)
-        deal(on_vector, w_scale[:], w_sraw[:], 16)
+        deal(on_vector, w_scale, w_scale_raw, 1)
         for first, width in X_PARTS:
             gather(3, first, width)
+
         weave_x(1, 0)
         weave_wg(0, 0, on_vector)
         weave_wg(0, 1, on_scalar)
@@ -259,42 +302,28 @@ def tile_list_relu_mix_noneP_kernel(
         quant_wg(0, 0, PASS // 2)
         quant_wg(0, PASS // 2, PASS // 2)
         weave_x(1, QUARTER)
-        up(0, 0)
         quant_x(1)
-        up(0, SUB)
-        weave_x(1, HALF)
-        up(0, 2 * SUB)
-        weave_x(1, HALF + QUARTER)
-        up(0, 3 * SUB)
-        quant_x(2)
-        weave_wg(1, 0, on_vector)
-        up(0, 4 * SUB)
-        weave_wg(1, 1, on_scalar)
-        quant_h(0, 0)
-        up(0, 5 * SUB)
-        deal(on_scalar, wu_codes[1][:], wu_raw[1][:], 4)
-        quant_wg(1, 0, PASS)
-        up(0, 6 * SUB)
-        deal(on_scalar, wd8_codes[:], wd8_raw[:], 4)
-        up(0, 7 * SUB)
-        deal(on_scalar, wd4_codes[:], wd4_raw[:], 8)
-        for c in range(NCH):
-            for first in range(STARTS[c], STARTS[c] + WIDTHS[c], SUB):
-                up(1, first)
-                if first == STARTS[c]:
-                    if c == 0:
-                        quant_h(0, 1)
-                    else:
-                        quant_h(1, c - 1)
-                        down(c - 1)
-        quant_h(1, NCH - 1)
-        down(NCH - 1)
+
+        steps = [(0, q) for q in range(3)] + [(1, 0), (0, 3)] + [(1, q) for q in range(1, 4)]
+        preparations = [prepare_upper_first_stage, prepare_second_stage]
+        previous = None
+        for k, (b, q) in enumerate(steps):
+            make_gate(b, q * QUARTER)
+            for first in range(q * QUARTER, (q + 1) * QUARTER, SUB):
+                make_h(b, first)
+                if previous is not None:
+                    finish_h(*previous)
+                previous = (b, first)
+            if k < len(preparations):
+                preparations[k]()
+        finish_h(*previous)
+
         weave_y(0, on_scalar)
-        for c in range(1, NCH):
+        for c in range(1, len(Y_PARTS)):
             weave_y(c, on_vector)
             quant_y(c - 1)
-        quant_y(NCH - 1)
-        y_sc = out_2[0].bitcast(I32)
+        quant_y(len(Y_PARTS) - 1)
+        y_scale_rows = out_2[0].bitcast(I32)
         for q in range(4):
             queue = nc.scalar if q % 2 else nc.sync
-            queue.dma_start(out=y_sc[4 * q : 4 * q + 4, :], in_=y_scale[32 * q : 32 * q + 4, :].bitcast(I32))
+            queue.dma_start(out=y_scale_rows[4 * q : 4 * q + 4, :], in_=y_scale[32 * q : 32 * q + 4, :].bitcast(I32))

from contextlib import ExitStack

import concourse.mybir as mybir

K, R, N, T, J = 512, 1024, 512, 2048, 1024
FLOPS = 2 * K * R * J * 2 + 2 * R * N * J

F32 = mybir.dt.float32
BF16 = mybir.dt.bfloat16
I32 = mybir.dt.int32
U32 = mybir.dt.uint32
U16 = mybir.dt.uint16
U8 = mybir.dt.uint8
FP8X4 = mybir.dt.float8_e4m3fn_x4
FP4X4 = mybir.dt.float4_e2m1fn_x4
MULT = mybir.AluOpType.mult
RELU = mybir.ActivationFunctionType.Relu

P = 128
PACK = 4
PASS = P * PACK
BANK = 512
LINE = 16
LIST_ROWS = 16
SUB = BANK // PACK
HALF = J // 2
QUARTER = J // 4

X_PARTS = [(0, QUARTER), (QUARTER, QUARTER), (HALF, HALF)]
Y_PARTS = [(0, QUARTER), (QUARTER, QUARTER), (HALF, QUARTER), (J - 2 * SUB, SUB), (J - SUB, SUB)]
H_PARTS = [[(0, HALF), (HALF, HALF)], Y_PARTS]

WD4_ROW, WU_ROWS, WD8_ROW = 0, (4, 8), 12


def part_of(parts, col):
    g = max(k for k, (first, width) in enumerate(parts) if first <= col)
    return g, col - parts[g][0]


def tile_list_relu_mix_noneP_kernel(
    tc, xT, wgt, wg, wu_words, wu_scales, wd8_words, wd8_scales, wd4_words, wd4_scales, offs, out_0, out_1, out_2
):
    nc = tc.nc
    on_vector, on_scalar = nc.vector.tensor_copy, nc.scalar.copy
    with ExitStack() as ctx:
        keep = ctx.enter_context(tc.tile_pool(name="keep", bufs=1))
        ring = ctx.enter_context(tc.tile_pool(name="ring", bufs=3))
        ps_ga = ctx.enter_context(tc.psum_pool(name="ps_ga", bufs=3))
        ps_ub = ctx.enter_context(tc.psum_pool(name="ps_ub", bufs=3))
        ps_y = ctx.enter_context(tc.psum_pool(name="ps_y", bufs=2))

        def part_tiles(name, parts, dtype, per_column=1):
            return [
                keep.tile([P, width * per_column], dtype, name="%s%d" % (name, g), align_bytes=64)
                for g, (first, width) in enumerate(parts)
            ]

        offsets = keep.tile([P, J // LIST_ROWS], U16, name="offsets")
        wgt_sb = [keep.tile([P, HALF], F32, name="wgt_sb%d" % u) for u in range(2)]
        x_rows = xT.rearrange("(p i) t -> p i t", i=PACK)
        x_sb = [keep.tile([P, T], F32, name="x_sb%d" % i) for i in range(PACK)]
        wg_rows = wg.rearrange("(p i) r -> p i r", i=PACK)
        wg_raw = [keep.tile([P, PACK, PASS], F32, name="wg_raw%d" % b) for b in range(2)]
        wu_raw = [keep.tile([P, PASS], U32, name="wu_raw%d" % b) for b in range(2)]
        wd8_raw = keep.tile([P, N], U32, name="wd8_raw")
        wd4_raw = keep.tile([P, N], U16, name="wd4_raw")
        w_scale_raw = keep.tile([P, PASS], U8, name="w_scale_raw")
        nc.vector.memset(w_scale_raw[:].bitcast(I32), 0)

        wu_src = wu_words[0].rearrange("p r i -> p (r i)").bitcast(I32)
        wu_scale_src = wu_scales[0].bitcast(I32).rearrange("q (b w) -> b q w", b=2)

        def load_x(i):
            nc.sync.dma_start(out=x_sb[i][:], in_=x_rows[:, i, :])

        def load_wgt(u):
            nc.sync.dma_start(out=wgt_sb[u][:], in_=wgt[:, u * HALF : (u + 1) * HALF])

        def load_wg(b):
            nc.sync.dma_start(out=wg_raw[b][:], in_=wg_rows[:, :, b * PASS : (b + 1) * PASS])

        def load_wu(b):
            nc.sync.dma_start(out=wu_raw[b][:].bitcast(I32), in_=wu_src[:, b * PASS : (b + 1) * PASS])

        def load_wu_scales(q):
            first = 32 * q + WU_ROWS[0]
            nc.sync.dma_start(out=w_scale_raw[first : first + 8, :].bitcast(I32), in_=wu_scale_src[:, 4 * q : 4 * q + 4, :])

        def load_wd_scales(queue, scales, row, q):
            first = 32 * q + row
            queue.dma_start(out=w_scale_raw[first : first + 4, :].bitcast(I32), in_=scales[0].bitcast(I32)[4 * q : 4 * q + 4, :])

        nc.sync.dma_start(offsets[:], offs)
        load_wgt(0)
        load_x(0)
        load_wgt(1)
        load_x(1)
        for q in range(3):
            load_wu_scales(q)
        load_x(2)
        load_wu_scales(3)
        for q in range(4):
            load_wd_scales(nc.sync, wd8_scales, WD8_ROW, q)
        load_wu(0)
        load_x(3)
        load_wg(0)
        load_wu(1)
        load_wg(1)
        nc.sync.dma_start(out=wd8_raw[:].bitcast(I32), in_=wd8_words[0].rearrange("p n i -> p (n i)").bitcast(I32))
        nc.sync.dma_start(out=wd4_raw[:].bitcast(I32), in_=wd4_words[0].bitcast(I32))
        for q in range(4):
            load_wd_scales(nc.gpsimd, wd4_scales, WD4_ROW, q)

        picked = [[keep.tile([P, 2, HALF], F32, name="picked%d_%d" % (pair, u)) for u in range(2)] for pair in range(2)]
        xg_bf = part_tiles("xg_bf", X_PARTS, BF16, PACK)
        xg_codes = part_tiles("xg_codes", X_PARTS, U32)
        xg_scale = part_tiles("xg_scale", X_PARTS, U8)

        def gather(i, first, width):
            u, at = divmod(first, HALF)
            nc.vector.tensor_tensor(
                picked[i // 2][u][:, i % 2, at : at + width],
                x_sb[i][:].indirect(offsets[:, first // LIST_ROWS : (first + width) // LIST_ROWS]),
                wgt_sb[u][:, at : at + width],
                MULT,
            )

        def weave_x(pair, first):
            u, at = divmod(first, HALF)
            g, to = part_of(X_PARTS, first)
            nc.scalar.copy(
                out=xg_bf[g][:, to * PACK : (to + QUARTER) * PACK].rearrange("p (g e u i) -> p u g i e", e=2, u=2, i=2)[:, pair],
                in_=picked[pair][u][:, :, at : at + QUARTER].rearrange("p i (g e) -> p g i e", e=2),
            )

        def quant_x(g):
            nc.vector.quantize_mx(out=xg_codes[g][:].bitcast(FP8X4), scales=xg_scale[g][:], in_=xg_bf[g][:])

        wg_bf = [keep.tile([P, PASS * PACK], BF16, name="wg_bf%d" % b, align_bytes=64) for b in range(2)]
        wg_codes = [keep.tile([P, PASS], U32, name="wg_codes%d" % b, align_bytes=64) for b in range(2)]
        wg_scale = [keep.tile([P, PASS], U8, name="wg_scale%d" % b, align_bytes=64) for b in range(2)]
        wu_codes = [keep.tile([P, PASS], U32, name="wu_codes%d" % b, align_bytes=64) for b in range(2)]
        w_scale = keep.tile([P, PASS], U8, name="w_scale", align_bytes=64)
        wd8_codes = keep.tile([P, N], U32, name="wd8_codes", align_bytes=64)
        wd4_codes = keep.tile([P, N], U16, name="wd4_codes", align_bytes=64)

        def weave_wg(b, u, copy):
            copy(
                out=wg_bf[b][:].rearrange("p (u t g e i) -> p u g e i t", u=2, t=2, e=2, i=PACK)[:, u],
                in_=wg_raw[b][:].rearrange("p i (g e u t) -> p u g e i t", u=2, t=2, e=2)[:, u],
            )

        def quant_wg(b, first, width):
            cols = slice(first, first + width)
            nc.vector.quantize_mx(
                out=wg_codes[b][:, cols].bitcast(FP8X4),
                scales=wg_scale[b][:, cols],
                in_=wg_bf[b][:, first * PACK : (first + width) * PACK],
            )

        def deal(copy, dst, src, element_bytes):
            run = LINE // element_bytes
            copy(
                out=dst[:].rearrange("p (t g e) -> p g t e", t=PACK, e=run),
                in_=src[:].rearrange("p (g e t) -> p g t e", t=PACK, e=run),
            )

        h_bf = [part_tiles("h_bf%d_" % b, H_PARTS[b], BF16, PACK) for b in range(2)]
        h_codes = [part_tiles("h_codes%d_" % b, H_PARTS[b], U32) for b in range(2)]
        h_scale = [part_tiles("h_scale%d_" % b, H_PARTS[b], U8) for b in range(2)]
        gate = {}

        def make_gate(b, first):
            gx, at = part_of(X_PARTS, first)
            cols = slice(at, at + QUARTER)
            gate[b, first] = ring.tile([P, PACK, QUARTER], F32, name="gate")
            for u in range(2):
                ga = ps_ga.tile([P, 2, QUARTER], F32, name="ga")
                for e in range(2):
                    t = 2 * u + e
                    nc.tensor.matmul_mx(
                        out=ga[:, e, :],
                        lhsT=wg_codes[b][:, t * P : (t + 1) * P].bitcast(FP8X4),
                        lhsT_scale=wg_scale[b][:, t * P : (t + 1) * P],
                        rhs=xg_codes[gx][:, cols].bitcast(FP8X4),
                        rhs_scale=xg_scale[gx][:, cols],
                        start=True,
                        stop=True,
                    )
                nc.scalar.activation(out=gate[b, first][:, 2 * u : 2 * u + 2, :], in_=ga[:], func=RELU)

        def make_h(b, first):
            gx, at = part_of(X_PARTS, first)
            gh, to = part_of(H_PARTS[b], first)
            cols = slice(at, at + SUB)
            ub = ps_ub.tile([P, PACK, SUB], F32, name="ub")
            for t in range(PACK):
                nc.tensor.matmul_mx(
                    out=ub[:, t, :],
                    lhsT=wu_codes[b][:, t * P : (t + 1) * P].bitcast(FP8X4),
                    lhsT_scale=w_scale[WU_ROWS[b] : P, t * P : (t + 1) * P],
                    rhs=xg_codes[gx][:, cols].bitcast(FP8X4),
                    rhs_scale=xg_scale[gx][:, cols],
                    start=True,
                    stop=True,
                )
            off = first % QUARTER
            nc.vector.tensor_tensor(
                h_bf[b][gh][:, to * PACK : (to + SUB) * PACK].rearrange("p (g e t) -> p g t e", e=4, t=PACK),
                ub[:].rearrange("p t (g e) -> p g t e", e=4),
                gate[b, first - off][:, :, off : off + SUB].rearrange("p t (g e) -> p g t e", e=4),
                MULT,
            )

        y_rows = out_0.rearrange("(p t) j -> p t j", t=PACK)
        y_words = out_1[0].rearrange("p j i -> p (j i)").bitcast(I32)
        y_scale = keep.tile([P, J], U8, name="y_scale", align_bytes=64)
        y_codes = keep.tile([P, J], U32, name="y_codes", align_bytes=64)
        y_sb = [keep.tile([P, PACK, width], F32, name="y_sb%d" % c) for c, (first, width) in enumerate(Y_PARTS)]
        y_bf = part_tiles("y_bf", Y_PARTS, BF16, PACK)

        def make_y(c):
            first, width = Y_PARTS[c]
            per_bank = BANK // width
            g0, at = part_of(H_PARTS[0], first)
            for t0 in range(0, PACK, per_bank):
                acc = ps_y.tile([P, per_bank, width], F32, name="acc")
                for t in range(t0, t0 + per_bank):
                    nc.tensor.matmul_mx(
                        out=acc[:, t - t0, :],
                        lhsT=wd8_codes[:, t * P : (t + 1) * P].bitcast(FP8X4),
                        lhsT_scale=w_scale[WD8_ROW:P, t * P : (t + 1) * P],
                        rhs=h_codes[0][g0][:, at : at + width].bitcast(FP8X4),
                        rhs_scale=h_scale[0][g0][:, at : at + width],
                        start=t == t0,
                        stop=False,
                    )
                for t in range(t0, t0 + per_bank):
                    nc.tensor.matmul_mx(
                        out=acc[:, t - t0, :],
                        lhsT=wd4_codes[:, t * P : (t + 1) * P].bitcast(FP4X4),
                        lhsT_scale=w_scale[WD4_ROW:P, t * P : (t + 1) * P],
                        rhs=h_codes[1][c][:].bitcast(FP8X4),
                        rhs_scale=h_scale[1][c][:],
                        start=False,
                        stop=t == t0 + per_bank - 1,
                    )
                nc.scalar.copy(out=y_sb[c][:, t0 : t0 + per_bank, :], in_=acc[:])
            nc.sync.dma_start(out=y_rows[:, :, first : first + width], in_=y_sb[c][:])

        def finish_h(b, first):
            g, to = part_of(H_PARTS[b], first)
            if to + SUB == H_PARTS[b][g][1]:
                nc.vector.quantize_mx(out=h_codes[b][g][:].bitcast(FP8X4), scales=h_scale[b][g][:], in_=h_bf[b][g][:])
                if b == 1:
                    make_y(g)

        def weave_y(c, copy):
            copy(
                out=y_bf[c][:].rearrange("p (g e t) -> p g t e", e=2, t=PACK),
                in_=y_sb[c][:].rearrange("p t (g e) -> p g t e", e=2),
            )

        def quant_y(c):
            first, width = Y_PARTS[c]
            cols = slice(first, first + width)
            nc.vector.quantize_mx(out=y_codes[:, cols].bitcast(FP8X4), scales=y_scale[:, cols], in_=y_bf[c][:])
            if cols.stop % HALF == 0:
                half = slice(cols.stop - HALF, cols.stop)
                nc.sync.dma_start(out=y_words[:, half], in_=y_codes[:, half].bitcast(I32))

        def prepare_upper_first_stage():
            weave_wg(1, 0, on_vector)
            weave_wg(1, 1, on_scalar)
            weave_x(1, HALF)
            weave_x(1, HALF + QUARTER)
            quant_x(2)
            quant_wg(1, 0, PASS)
            deal(on_scalar, wu_codes[1], wu_raw[1], 4)

        def prepare_second_stage():
            deal(on_scalar, wd8_codes, wd8_raw, 4)
            deal(on_scalar, wd4_codes, wd4_raw, 2)

        for i in range(2):
            for first in (0, HALF):
                gather(i, first, HALF)
        for first in range(0, J, QUARTER):
            weave_x(0, first)
        deal(on_scalar, wu_codes[0], wu_raw[0], 4)
        for first in (0, HALF):
            gather(2, first, HALF)
        deal(on_vector, w_scale, w_scale_raw, 1)
        for first, width in X_PARTS:
            gather(3, first, width)

        weave_x(1, 0)
        weave_wg(0, 0, on_vector)
        weave_wg(0, 1, on_scalar)
        quant_x(0)
        quant_wg(0, 0, PASS // 2)
        quant_wg(0, PASS // 2, PASS // 2)
        weave_x(1, QUARTER)
        quant_x(1)

        steps = [(0, q) for q in range(3)] + [(1, 0), (0, 3)] + [(1, q) for q in range(1, 4)]
        preparations = [prepare_upper_first_stage, prepare_second_stage]
        previous = None
        for k, (b, q) in enumerate(steps):
            make_gate(b, q * QUARTER)
            for first in range(q * QUARTER, (q + 1) * QUARTER, SUB):
                make_h(b, first)
                if previous is not None:
                    finish_h(*previous)
                previous = (b, first)
            if k < len(preparations):
                preparations[k]()
        finish_h(*previous)

        weave_y(0, on_scalar)
        for c in range(1, len(Y_PARTS)):
            weave_y(c, on_vector)
            quant_y(c - 1)
        quant_y(len(Y_PARTS) - 1)
        y_scale_rows = out_2[0].bitcast(I32)
        for q in range(4):
            queue = nc.scalar if q % 2 else nc.sync
            queue.dma_start(out=y_scale_rows[4 * q : 4 * q + 4, :], in_=y_scale[32 * q : 32 * q + 4, :].bitcast(I32))
